import numpy as np, ml_dtypes
CORES = [113,118,241,246]
N = 4
BF = ml_dtypes.bfloat16
def gentries(a):
    return np.ascontiguousarray(a.reshape(8, 16, -1).transpose(0, 2, 1)).reshape(8, -1)
def gtable(e):
    e = np.asarray(e); return np.ascontiguousarray(e.reshape(8, -1, 16).transpose(0, 2, 1)).reshape(128, -1).astype(np.int32)
L, E, H, RO = 3, 384, 2, 2
V = L * E; W = (1 + H) * V
def feed(rng, far, void):
    x = rng.integers(V, W, (N, 8, 16, V))
    for l in range(1, L):
        s = slice(l * E, (l + 1) * E); own = rng.integers(0, l * E, (N, 8, 16, E))
        x[..., s] = np.where(rng.random(own.shape) < far, x[..., s], own)
    return np.where(rng.random(x.shape) < void, -1, x)
def edges(rng):
    x = np.zeros((N, 8, 16, V), np.int64)
    for l in range(L):
        few = np.array(([0, l * E - 1, V, W - 1] if l else [V, 2 * V - 1, W - 1]) + ([2 * V, H * V] if H > 1 else []))
        x[..., l * E:(l + 1) * E] = rng.choice(few, (N, 8, 16, E))
    return x
def links(rng):
    return np.argsort(rng.random((N, 8, L, E)), axis=-1).reshape(N, 8, V)
def first(rng, empty):
    cf = rng.integers(V, W, (N, 8, E))
    return np.where(rng.random(cf.shape) < empty, -1, cf), rng.integers(0, 17, (N, 8, E))
def near(rng, base):
    return np.clip(base + rng.integers(-20, 21, (N, 8, 16, V)), 0, 255)
def pack(fd, pw, bs, dl, nx, t0, cf, cw):
    def lanes(a): return np.ascontiguousarray(a.reshape(N, 128, V)).astype(np.float32).astype(BF)
    return {"fd": np.ascontiguousarray(fd.reshape(N, 128, V)).astype(np.int32), "pw": lanes(pw), "bs": lanes(bs), "t0": lanes(t0),
            "dl": dl.astype(np.int32), "nx": np.stack([gtable(a) for a in nx]), "cf": cf.astype(np.int32), "cw": cw.astype(np.int32)}
def setup_inputs(rng):
    base = rng.integers(0, 236, (N, 8, 1, V)); void = rng.choice(np.array([0.0, 0.05, 0.2, 0.7]), (N, 8, 1, V))
    pw = np.minimum((17 * rng.random((N, 8, 16, V)) ** 2).astype(np.int64), 16)
    pw = np.where(rng.random((N, 8, 1, V)) < 0.125, pw[:, :, :1], pw)
    cf, cw = first(rng, 0.25)
    return pack(feed(rng, 0.4, void), pw, near(rng, base), rng.integers(1, 5, (N, 8, V)), links(rng), near(rng, base), cf, cw)
def setup_inputs_spread(rng):
    bs = np.minimum((np.exp2(8 * rng.random((N, 8, 1, V))) * rng.random((N, 8, 16, V))).astype(np.int64), 255)
    t0 = np.minimum((np.exp2(8 * rng.random((N, 8, 1, V))) * rng.random((N, 8, 16, V))).astype(np.int64), 255)
    bs = np.where(rng.random(bs.shape) < 0.02, 255, bs); t0 = np.where(rng.random(t0.shape) < 0.02, 255, t0)
    pw = np.minimum((17 * rng.random((N, 8, 16, V)) ** rng.choice(np.array([0.5, 1.0, 3.0, 8.0]), (N, 8, 1, V))).astype(np.int64), 16)
    x = feed(rng, rng.choice(np.array([0.05, 0.5, 0.95]), (N, 8, 1, 1)), rng.random((N, 8, 1, V)) ** 2)
    crowd = V + ((x - V) * rng.random(x.shape) ** 3).astype(np.int64)
    x = np.where((x >= V) & (np.arange(8)[None, :, None, None] % 2 == 1), crowd, x)
    cf, cw = first(rng, 0.4)
    return pack(x, pw, bs, rng.choice(np.array([1, 1, 1, 2, 3, 4]), (N, 8, V)), links(rng), t0, cf, cw)
def setup_inputs_ends(rng):
    def two():
        m = rng.choice(np.array([0, 1, 2]), (N, 8, 1, V), p=[0.45, 0.2, 0.35])
        return 255 * np.where(m == 2, rng.integers(0, 2, (N, 8, 16, V)), m)
    bs = two(); t0 = two()
    pw = 16 * (rng.random((N, 8, 16, V)) < rng.choice(np.array([0.0, 0.06, 1.0]), (N, 8, 1, V), p=[0.6, 0.3, 0.1])).astype(np.int64)
    u = rng.random((N, 8, 16, V)); x = np.where(u < 0.35, -1, np.where(u < 0.75, W - 1, edges(rng)))
    bs[N - 1, 7, :, V - 1] = 255; t0[N - 1, 7, :, V - 1] = 255; pw[N - 1, 7, :, V - 1] = 0
    t0[N - 1 - H, 7 - H, :, V - 1] = 255; bs[N - 1, 7, :, E - 1] = 0; t0[N - 1, 7, :, E - 1] = 0; pw[N - 1, 7, :, E - 1] = 0; x[N - 1, 7, :, E - 1] = W - 1
    mid = 1 + np.argsort(rng.random((N, 8, L, E - 2)), axis=-1); one = np.ones((N, 8, L, 1), np.int64)
    nx = np.where(rng.random((N, 8, L, 1)) < 0.5, np.arange(E)[::-1], np.concatenate([(E - 1) * one, mid, 0 * one], axis=-1))
    c = rng.random((N, 8, E)); cf = np.where(c < 0.45, -1, np.where(c < 0.85, W - 1, V)); cf[N - 1, 7, E - 1] = W - 1
    return pack(x, pw, bs, 1 + 3 * rng.integers(0, 2, (N, 8, V)), nx.reshape(N, 8, V), t0, cf, 16 * rng.integers(0, 2, (N, 8, E)))
def setup_inputs_corners(rng):
    kd = np.argsort(rng.random((N, 8)), axis=1)[:, :, None, None]; ke = kd[..., 0]
    base = rng.integers(0, 236, (N, 8, 1, V)); bs = near(rng, base); t0 = near(rng, base); e = rng.random((N, 8, 1, V))
    bs = np.where(e < 0.1, 0, np.where(e < 0.15, 255, bs)); t0 = np.where(e < 0.05, 0, np.where((e > 0.12) & (e < 0.2), 255, t0))
    nv = rng.choice(np.array([0, 1, 15, 16]), (N, 8, 1, V))
    for k, n in ((0, 0), (1, 16), (2, 0), (3, 1), (4, 15)): nv = np.where(kd == k, n, nv)
    x = np.where(kd == 5, edges(rng), feed(rng, 0.5, 0.0))
    x = np.where(np.argsort(rng.random((N, 8, 16, V)), axis=2) < nv, -1, x)
    pw = rng.integers(0, 17, (N, 8, 16, V))
    pw = np.where(kd == 3, pw[:, :, :1], np.where(kd == 5, 16 * rng.integers(0, 2, pw.shape), np.where(kd == 0, 16, np.where(kd == 2, 0, pw))))
    cf, cw = first(rng, 0.3); full, heavy = first(rng, 0.0)
    cf = np.where(ke == 1, -1, np.where((ke == 0) | (ke == 2) | (ke == 4), full, cf))
    cw = np.where(ke == 0, rng.choice(np.array([0, 15, 16]), cw.shape), np.where(ke == 2, 0, np.where(ke == 4, 16, cw)))
    return pack(x, pw, bs, rng.integers(1, 5, (N, 8, V)), links(rng), t0, cf, cw)
def setup_inputs_heavy(rng):
    late = np.arange(V) >= E
    bs = rng.integers(0, 201, (N, 8, 16, V)); t0 = rng.integers(1, 151, (N, 8, 16, V))
    low = late & (rng.random((N, 8, 1, V)) < 0.4); bs = np.where(low, 0, bs); t0 = np.where(low, 0, t0)
    n15 = rng.choice(np.array([0, 0, 1, 1, 2, 16]), (N, 8, 1, V))
    pw = np.where(np.argsort(rng.random((N, 8, 16, V)), axis=2) < n15, 15, 16)
    light = late & (rng.random((N, 8, 1, V)) < 0.75); pw = np.where(light, rng.integers(0, 15, pw.shape), pw)
    x = feed(rng, 0.5, np.where(light, 0.2, 0.0))
    cf, cw = first(rng, 0.1); cw = rng.choice(np.array([16, 16, 16, 15]), cw.shape)
    return pack(x, pw, bs, rng.integers(1, 5, (N, 8, V)), links(rng), t0, cf, cw)
def setup_inputs_ties(rng):
    lv = 3 * np.repeat(np.arange(L), E)
    bs = 60 + lv + rng.integers(0, 4, (N, 8, 16, V)); t0 = 60 + lv + rng.integers(0, 4, (N, 8, 16, V))
    lift = (rng.random((N, 8, 16, V)) < 0.3) & (rng.random((N, 8, 1, V)) < 0.5)
    pw = rng.choice(np.array([4, 8, 8, 9, 12, 15]), (N, 8, 1, V)) + lift.astype(np.int64)
    x = feed(rng, 0.5, rng.choice(np.array([0.0, 0.0, 0.1]), (N, 8, 1, V)))
    cf, cw = first(rng, 0.1); cw = rng.choice(np.array([4, 8, 9, 12]), cw.shape)
    return pack(x, pw, bs, 1 + 3 * (rng.random((N, 8, V)) < 0.2).astype(np.int64), links(rng), t0, cf, cw)
def check_inputs(d):
    bad = []
    for k, lo, hi in (("fd", -1, W - 1), ("pw", 0, 16), ("bs", 0, 255), ("t0", 0, 255), ("dl", 1, 4), ("nx", 0, E - 1), ("cf", -1, W - 1), ("cw", 0, 16)):
        a = np.asarray(d[k]).astype(np.float64)
        if not (np.all(a >= lo) and np.all(a <= hi) and np.all(a == np.floor(a))): bad.append("range of " + k)
    x = d["fd"].reshape(N, 128, L, E); c = d["cf"]
    if np.any((x < V) & (x >= (np.arange(L) * E)[None, None, :, None])): bad.append("own feeders of fd lie in earlier levels")
    if np.any((c >= 0) & (c < V)): bad.append("first carried feeders of cf are foreign")
    n = np.stack([gentries(a) for a in d["nx"]]).reshape(N, 8, L, E)
    if np.any(np.sort(n, axis=-1) != np.arange(E)): bad.append("nx is a permutation in each level")
    return bad
def reference(fd, pw, bs, t0, dl, nx, cf, cw):
    fe = fd.astype(np.int64).reshape(N, 8, 16, V); wt = np.where(fe < 0, -1, pw.astype(np.float32).astype(np.int64).reshape(N, 8, 16, V))
    base = bs.astype(np.float32).astype(np.int32).reshape(N, 8, 16, V); T = t0.astype(np.float32).astype(np.int32).reshape(N, 8, 16, V)
    to = np.stack([gentries(a) for a in nx]).astype(np.int64); dd = dl.astype(np.int32)[:, :, None, :]
    inf = cf.astype(np.int64); inw = np.where(inf < 0, -1, cw.astype(np.int64))
    rows = np.arange(16)[None, None, :, None]
    for q in range(RO):
        old = T.copy()
        win = np.concatenate([T] + [np.roll(old, (h, h), (0, 1)) for h in range(1, H + 1)], axis=3)
        for l in range(L):
            s = slice(l * E, (l + 1) * E); f = fe[..., s]; w = wt[..., s]
            m = np.argmin(w, axis=2)[:, :, None]
            lf = np.take_along_axis(f, m, 2)[:, :, 0]; lw = np.take_along_axis(w, m, 2)[:, :, 0]
            enter = inw > lw; put = enter[:, :, None] & (rows == m)
            hf = np.where(enter, lf, inf); hw = np.where(enter, lw, inw)
            f = np.where(put, inf[:, :, None], f); w = np.where(put, inw[:, :, None], w)
            b = (base[..., s] + old[..., s]) >> 1
            a = np.take_along_axis(win, np.maximum(f, 0).reshape(N, 8, 1, 16 * E), 3).reshape(N, 8, 16, 16, E)
            c = np.add.reduce(a > b[:, :, :, None], axis=2, dtype=np.int64)
            drop = c > w
            t = np.max(np.where(drop[:, :, None], 0, a), axis=3)
            T[..., s] = np.minimum(255, np.maximum(b, t) + dd[..., s]); win[..., s] = T[..., s]
            v = np.where(drop, w, -1); m = np.argmax(v, axis=2)[:, :, None]
            gf = np.take_along_axis(f, m, 2)[:, :, 0]; gw = np.take_along_axis(v, m, 2)[:, :, 0]
            take = gw > hw; gone = take[:, :, None] & (rows == m)
            outf = np.where(take, gf, hf); outw = np.where(take, gw, hw)
            fe[..., s] = np.where(gone, -1, f); wt[..., s] = np.where(gone, -1, w)
            if l == L - 1: outf = np.where(outw < 0, -1, V + l * E + np.arange(E))
            inf = np.zeros_like(outf); inw = np.zeros_like(outw)
            np.put_along_axis(inf, to[..., s], outf, 2); np.put_along_axis(inw, to[..., s], outw, 2)
            if l == L - 1: inf = np.roll(inf, (1, 1), (0, 1)); inw = np.roll(inw, (1, 1), (0, 1))
    return {"yt": np.ascontiguousarray(T.reshape(N, 128, V)).astype(np.float32).astype(BF)}

@@ -1,0 +1,730 @@
+import math
+import numpy as np
+from concourse.bass import DstId, RemoteDMATransfer
+from concourse.mybir import AluOpType, ActivationFunctionType
+
+ALU = AluOpType
+AF = ActivationFunctionType
+E, HE, V, W3 = 384, 192, 1152, 3456
+R = 57344.0
+BETA, ALPHA = 40.0, 1.5
+CL = math.log(BETA)
+LNK = 114 * math.log(2.0)
+MAGIC = 12582912.0
+PAIR = False
+NW = 8
+NS = NW + 1
+GCH = 4
+NX = 0
+KF = 1048576.0
+K2 = 24 * math.log(2.0)
+NG_ACT = True
+QDMA = True
+VGATHER = {(0, 1), (0, 3)}
+TRIES = 600
+CSPLIT, NSPLIT = 96, 16
+
+SCRATCH = {
+    "fdn": ("sbuf", [128, E], "int32"), "ffn": ("sbuf", [128, E], "float32"), "ngn": ("sbuf", [128, E], "bfloat16"),
+    "pwn": ("sbuf", [128, E], "bfloat16"), "bsn": ("sbuf", [128, V], "bfloat16"),
+    "fds": ("sbuf", [128, 4 * HE], "int32"), "pws": ("sbuf", [128, 4 * HE], "bfloat16"), "kf": ("sbuf", [128, 4 * HE], "float32"),
+    "idk": ("sbuf", [128, 128], "float32"), "prb": ("sbuf", [128, 128], "bfloat16"),
+    "nxn": ("sbuf", [128, 72], "int32"), "nxf": ("sbuf", [128, 72], "float32"),
+    "dln": ("sbuf", [128, E], "int32"), "dlb": ("sbuf", [128, E], "bfloat16"),
+    "c3n": ("sbuf", [128, E], "int32"), "c3f": ("sbuf", [128, E], "float32"), "ab": ("sbuf", [128, 8], "float32"),
+    "one": ("sbuf", [128, 256], "bfloat16"), "cst": ("sbuf", [128, 384], "bfloat16"),
+    "ui": ("sbuf", [128, 8], "int32"), "uf": ("sbuf", [128, 8], "float32"), "uq": ("sbuf", [128, 16], "float32"),
+    "vp": ("sbuf", [128, 128], "bfloat16"), "vb": ("sbuf", [128, 128], "bfloat16"), "vj": ("sbuf", [128, 128], "bfloat16"),
+    "v16": ("sbuf", [128, 256], "int32"), "vg": ("sbuf", [128, 256], "int32"), "v3": ("sbuf", [128, 512], "bfloat16"),
+    "ib": ("sbuf", [128, 128], "bfloat16"), "nib": ("sbuf", [128, 128], "bfloat16"), "nrb": ("sbuf", [128, 128], "bfloat16"),
+    "idf": ("sbuf", [128, 128], "float32"), "blk": ("sbuf", [128, 128], "float32"), "nblk": ("sbuf", [128, 128], "float32"),
+    "tt1": ("sbuf", [128, 128], "float32"), "tt2": ("sbuf", [128, 128], "float32"), "tri": ("sbuf", [128, 128], "bfloat16"),
+    "cwin": ("sbuf", [128, 144], "bfloat16"), "pen": ("sbuf", [128, 2048], "bfloat16"),
+    "wb": ("sbuf", [128, 17 * 64], "bfloat16"), "wf": ("sbuf", [128, 13 * 64], "float32"),
+    "rep": ("sbuf", [128, 512], "bfloat16"), "dsel": ("sbuf", [128, 12 * 128], "bfloat16"),
+    "ec": ("sbuf", [128, HE], "float32"), "cmp": ("sbuf", [128, 3072], "bfloat16"),
+}
+if PAIR:
+    SCRATCH["rst"] = ("sbuf", [128, HE, NS], "bfloat16")
+else:
+    SCRATCH["rst"] = ("sbuf", [128, HE * NS], "bfloat16")
+for _s in (0, 1):
+    for _n, _w, _d in (("wa", W3, "bfloat16"), ("wc", W3, "bfloat16"), ("rb", V, "bfloat16"), ("ga", 3072, "bfloat16"),
+                       ("q", 3 * HE, "float32"), ("qn", HE, "float32"), ("qb", 3 * HE, "float32"), ("gn", HE, "float32"), ("iq", HE, "float32"), ("iz", HE, "float32"),
+                       ("isd", HE, "float32"), ("en", HE, "bfloat16"), ("ei", HE, "bfloat16"), ("wn", HE, "bfloat16"),
+                       ("of", HE, "uint16"), ("hq", HE, "float32"), ("eh", HE, "bfloat16"), ("ed", HE, "bfloat16"),
+                       ("dr", HE, "bfloat16"), ("ou", HE, "float32"), ("rw", HE, "float32"), ("wo", HE, "bfloat16"),
+                       ("sc", 3 * E, "float32"), ("nxo", 36, "uint16")):
+        SCRATCH["%s%d" % (_n, _s)] = ("sbuf", [128, _w], _d)
+    for _n in ("sl", "so"):
+        SCRATCH["%s%d" % (_n, _s)] = ("sbuf", [128, HE, NS] if PAIR else [128, HE * NS], "bfloat16")
+for _b in range(8):
+    SCRATCH["ps%d" % _b] = ("psum", [128, 512], "float32")
+SEMAPHORES = ["eV", "eA", "eP", "eG", "arr0", "arr1", "arr2", "arr3"] + ["d%d" % _i for _i in range(48)] + ["l%d" % _i for _i in range(12)]
+
+IO_SHAPES = {"fd": [128, V], "pw": [128, V], "bs": [128, V], "t0": [128, V], "yt": [128, V], "nx": [128, 72],
+             "dl": [8, V], "cf": [8, E], "cw": [8, E]}
+WIDTH = {"float32": 4, "int32": 4, "bfloat16": 2, "uint16": 2}
+ALL = slice(None)
+
+
+def work(us=0.0, vi=0.0, cyc=0.0, ga=0.0, sc=0.0, pi=0.0, pe=0.0):
+    return np.array([us, vi, cyc, ga, sc, pi, pe])
+
+
+def rates(f, vi, ga, sc, pi, pe, lat):
+    return np.array([1.0, vi, 0.00083 * f, 0.00083 * f * ga, 0.00083 * f * sc, pi, pe * f]), lat
+
+
+RATES = [rates(1.25, 0.04, 1.56, 3.8, 0.01, 0.00042, 0.1), rates(1.05, 0.02, 1.15, 2.2, 0.0, 0.00042, 0.06),
+         rates(1.4, 0.05, 1.95, 5.2, 0.01, 0.00042, 0.18)]
+
+
+def ap(name, *idx):
+    return ("ap", name, tuple(idx) if idx else (ALL,))
+
+
+def cols(name, a, b, step=None, p=ALL):
+    return ap(name, p, slice(a, b, step))
+
+
+def ind(win, off):
+    return ("ind", win, off)
+
+
+def slot(name, j, n=1):
+    if PAIR:
+        return ap(name, ALL, ALL, slice(j, j + n)) if n > 1 else ap(name, ALL, ALL, j)
+    return cols(name, j, HE * NS, NS)
+
+
+_REG = {}
+
+
+def region(a):
+    key = repr(a)
+    if key not in _REG:
+        name, idx = a[1], a[2]
+        shape = SCRATCH[name][1] if name in SCRATCH else IO_SHAPES[name]
+        p = range(shape[0])[idx[0]]
+        c = np.arange(int(np.prod(shape[1:]))).reshape(shape[1:])[idx[1:]].ravel()
+        m = 0
+        for x in c.tolist():
+            m |= 1 << x
+        _REG[key] = (name, p[0], p[-1] + 1, m, len(c))
+    return _REG[key]
+
+
+def two_bytes(aps):
+    return all(WIDTH[SCRATCH[a[1]][2]] == 2 for a in aps)
+
+
+def in_psum(a):
+    return a[1].startswith("ps")
+
+
+def build(rank, core, cores, topo):
+    ops = []
+    tag = [0]
+
+    def add(eng, calls, reads, writes, cost, **kw):
+        rd = []
+        for a in reads:
+            rd += [a[1], a[2]] if a[0] == "ind" else [a]
+        wr = []
+        for a in writes:
+            if a[0] == "ind":
+                wr.append(a[1]); rd.append(a[2])
+            else:
+                wr.append(a)
+        o = dict(eng=eng, calls=calls, rd=[region(a) for a in rd], wr=[region(a) for a in wr], cost=cost, hold=cost,
+                 kind="c", arr=None, acc=False, tag=tag[0])
+        o.update(kw)
+        o["banks"] = set(x[0] for x in o["rd"] + o["wr"] if x[0].startswith("ps"))
+        ops.append(o)
+        return o
+
+    def nel(a):
+        return 16 * region(a[2])[4] if a[0] == "ind" else region(a)[4]
+
+    def aps(*xs):
+        return [x for x in xs if isinstance(x, tuple)]
+
+    def vcost(out, ins, f=1.0):
+        if out[0] == "ind":
+            return work(vi=1, sc=nel(out))
+        if ins[0][0] == "ind":
+            return work(vi=1, ga=nel(out))
+        return work(vi=1, cyc=max(64, nel(out) * f))
+
+    def ts(out, in0, s1, s2, op0, op1=None, **kw):
+        args = (out, in0, s1, s2, op0) + ((op1,) if op1 is not None else ())
+        f = 0.5 if in0[0] == "ap" and out[0] == "ap" and two_bytes([out, in0]) else 1.0
+        return add("V", [("tensor_scalar", args, {})], aps(in0, s1, s2), [out], vcost(out, [in0], f), **kw)
+
+    def tt(out, in0, in1, op, **kw):
+        f = 1.0 if in0[0] == "ind" or in_psum(in0) or in_psum(in1) else 2.0
+        return add("V", [("tensor_tensor", (out, in0, in1, op), {})], [in0, in1], [out], vcost(out, [in0], f), **kw)
+
+    def cp(out, in_, **kw):
+        f = 0.5 if in_[0] == "ap" and out[0] == "ap" and two_bytes([out, in_]) else 1.0
+        return add("V", [("tensor_copy", (out, in_), {})], [in_], [out], vcost(out, [in_], f), **kw)
+
+    def mset(out, c):
+        return add("V", [("memset", (out, c), {})], [], [out], work(vi=1, cyc=max(64, nel(out) * (0.5 if two_bytes([out]) else 1.0))))
+
+    def act(out, in_, func, bias=None, scale=None, **kw):
+        k = {}
+        if bias is not None:
+            k["bias"] = float(bias)
+        if scale is not None:
+            k["scale"] = float(scale)
+        c = work(vi=1.3, ga=nel(out)) if in_[0] == "ind" else work(vi=1.3, cyc=max(64, nel(out)))
+        return add("A", [("activation", (out, in_, func), k)], [in_], [out], c, **kw)
+
+    def mm(terms, first=True, last=True, **kw):
+        calls, c, rd, wr = [], 0.0, [], []
+        for i, (out, l, r) in enumerate(terms):
+            calls.append(("matmul", (out, l, r, first and i == 0, last and i == len(terms) - 1), {}))
+            c = c + work(pi=1, pe=max(64, nel(r)) * (4 if SCRATCH[r[1]][2] == "float32" else 1))
+            rd += [l, r]; wr.append(out)
+        return add("P", calls, rd, wr, c, **kw)
+
+    def iota(out, pattern, base, cm):
+        k = {} if SCRATCH[out[1]][2] == "int32" else {"allow_small_or_imprecise_dtypes": True}
+        return add("G", [("iota", (out, pattern, base, cm), k)], [], [out], work(us=0.15, cyc=2 * nel(out)))
+
+    def sel(out, in_, pattern, op, fill, base, cm):
+        return add("G", [("affine_select", (out, in_, pattern, op, fill, base, cm), {})], [in_], [out], work(us=0.2, cyc=2 * nel(out)))
+
+    nd = [0]
+
+    def dma(eng, pairs, nbytes, accum=False):
+        s = "d%d" % nd[0]; nd[0] += 1
+        calls = [("dma_start", (o, i), {"accum_op": ALU.add} if accum else {}) for o, i in pairs]
+        return add(eng, calls, [i for o, i in pairs], [o for o, i in pairs], work(us=0.1 * len(pairs) + 1.9 + nbytes / 150e3),
+                   hold=work(us=(1.0 if eng == "G" else 0.1) * len(pairs)), kind="d", sem=s, total=16 * len(pairs))
+
+    dests = [cores[(rank + 1) % 4], cores[(rank + 2) % 4]]
+
+    def masks(src, ds):
+        lists = [topo.engines(src, d) for d in ds]
+        if len(ds) == 2 and len(lists[0]) == len(lists[1]):
+            h = len(lists[0]) // 2
+            lists = [lists[0][:h], lists[1][h:]]
+        elif len(ds) == 2:
+            big = 0 if len(lists[0]) > len(lists[1]) else 1
+            lists[big] = [e for e in lists[big] if e not in lists[1 - big]]
+        return [sum(1 << e for e in x) for x in lists], [len(x) for x in lists]
+
+    my_masks, my_n = masks(core, dests)
+    from1 = masks(cores[(rank - 1) % 4], [core, cores[(rank + 1) % 4]])[1][0]
+    from2 = masks(cores[(rank - 2) % 4], [cores[(rank - 1) % 4], core])[1][1]
+    arr_total = {0: from1 + from2, 1: from1 + from2, 2: 4 * from1 + 3 * from2, 3: 4 * from1 + 3 * from2}
+    nl = [0]
+
+    def remote(items, arr, nbytes):
+        s = "l%d" % nl[0]; nl[0] += 1
+        tr = [(topo.addr(dests[w], core), my_masks[w], src, dst) for w, src, dst in items]
+        return add("G", [("remote", tr, {})], [x[1] for x in items], [], work(us=2.5 + nbytes / 60e3), hold=work(us=0.3), kind="r", sem=s,
+                   total=sum(my_n[w] for w, _, _ in items), rsem="arr%d" % arr, sends=arr)
+
+    rolled = [(rank + 1) % 4 < rank, (rank + 2) % 4 < rank]
+
+    def grp(s_, s):
+        return (2 * s_ + (s & 1) + 4 * (s >> 1) + rank) % 8
+
+    def runs(s_, x):
+        out = []
+        for s in range(4):
+            gq = grp(s_, s ^ x)
+            if out and out[-1][1] + out[-1][2] == gq and s % 2 == 1:
+                out[-1][2] += 1
+            else:
+                out.append([s, gq, 1])
+        return out
+
+    def t0_pairs(buf, s_, x):
+        return [(ap(buf, slice(64 * h + 16 * s, 64 * h + 16 * (s + n)), slice(0, V)), ap("t0", slice(16 * gq, 16 * (gq + n)), ALL))
+                for h in (0, 1) for s, gq, n in runs(s_, x)]
+
+    for s_ in (0, 1):
+        if any(rolled):
+            dma("S" if s_ == 0 else "A", t0_pairs("rb%d" % s_, s_, 2), 295e3)
+        dma("A" if s_ == 0 else "S", t0_pairs("wa%d" % s_, s_, 0), 295e3)
+        if s_ == 0:
+            dma("S", [(cols("fdn", 0, E), cols("fd", 0, E))], 200e3)
+            dma("A", [(cols("pwn", 0, E), cols("pw", 0, E))], 100e3)
+            dma("S", [(ap("c3n", slice(0, 8), ALL), ap("cf")), (ap("c3n", slice(8, 16), ALL), ap("cw")),
+                      (ap("c3n", slice(16, 24), ALL), ap("cf"))], 40e3)
+        remote([(w, cols(("rb%d" if rolled[w] else "wa%d") % s_, 0, V), cols("wa%d" % s_, V * (w + 1), V * (w + 2))) for w in (0, 1)],
+               s_, 590e3)
+    dma("S", [(ap("bsn"), ap("bs"))], 295e3)
+    dma("S", [(ap("nxn"), ap("nx")), (ap("dln", slice(0, 24), ALL), ap("dl"))], 80e3)
+    for l in (1, 2):
+        for s_ in (0, 1):
+            a = HE * (2 * s_ + l - 1)
+            dma("S", [(ap(buf, slice(64 * h + 16 * s, 64 * h + 16 * (s + c)), slice(a, a + HE)),
+                       ap(src, slice(16 * gq, 16 * (gq + c)), slice(E * l + HE * h, E * l + HE * h + HE)))
+                      for buf, src in (("fds", "fd"), ("pws", "pw")) for h in (0, 1) for s, gq, c in runs(s_, 0)], 150e3)
+    for s_ in (0, 1):
+        dma("S", t0_pairs("wc%d" % s_, s_, 0), 295e3)
+
+    mset(ap("one"), 1.0)
+    mset(cols("cst", 0, 128), R); mset(cols("cst", 128, 256), -0.25)
+    mset(ap("wf"), 0.0); mset(ap("wb"), 0.0); mset(ap("cwin"), 0.0)
+    mset(cols("ab", 0, 1), 1.0); mset(cols("ab", 4, 5), 1e9)
+    iota(ap("uq"), [[-1, 16]], 0, 1)
+    iota(cols("ui", 0, 1), [[0, 1]], 0, 1)
+    iota(ap("vp"), [[1, 128]], 0, 0)
+    iota(ap("vb"), [[16, 8], [0, 16]], 0, 0)
+    for s_ in (0, 1):
+        iota(cols("v16", 64 * s_, 64 * s_ + 64), [[64, 2], [16, 2], [1, 16]], 16 * (2 * s_ + rank), 0)
+    nv = 128
+    p24 = slice(0, 24)
+    sel(ap("ab", p24, slice(0, 1)), ap("ab", p24, slice(0, 1)), [[0, 1]], ALU.is_gt, R, 8, -1)
+    sel(ap("ab", p24, slice(0, 1)), ap("ab", p24, slice(0, 1)), [[0, 1]], ALU.is_gt, 32 * R, 16, -1)
+    sel(ap("ab", p24, slice(4, 5)), ap("ab", p24, slice(4, 5)), [[0, 1]], ALU.is_gt, 0.0, 16, -1)
+    for j, m in ((1, 7), (2, 63), (3, 112)):
+        ts(cols("ui", j, j + 1), cols("ui", 0, 1), m, None, ALU.bitwise_and)
+    cp(cols("uf", 0, 4), cols("ui", 0, 4))
+    q0, u7, u63, u112 = cols("uq", 0, 1), cols("uf", 1, 2), cols("uf", 2, 3), cols("uf", 3, 4)
+
+    def eq(out, row, col, c):
+        return ts(out, row, col, float(c), ALU.is_equal, ALU.mult)
+
+    eq(ap("ib"), ap("vp"), q0, 1); eq(ap("nib"), ap("vp"), q0, -1); eq(ap("nrb"), ap("vp"), q0, -R); eq(ap("idf"), ap("vp"), q0, 1)
+    eq(ap("blk"), ap("vb"), u112, 1); eq(ap("nblk"), ap("vb"), u112, -1)
+    eq(cols("cwin", 15, 143, 16), cols("vb", 0, 128, 16), u112, 1)
+    c1, c2 = -ALPHA + ALPHA / BETA, -ALPHA / BETA
+    ts(ap("tt1"), ap("vp"), q0, c2 / c1, ALU.is_gt, ALU.add)
+    eq(ap("tt2"), ap("vb"), u112, c1)
+    tt(ap("tt1"), ap("tt1"), ap("tt2"), ALU.mult)
+    tt(ap("tri"), ap("tt1"), ap("idf"), ALU.add)
+    ts(cols("v16", 0, nv), cols("v16", 0, nv), 127, None, ALU.bitwise_and)
+    ts(cols("vg", 0, nv), cols("v16", 0, nv), 4, None, ALU.arith_shift_right)
+
+    def blkw(buf, j):
+        return cols(buf, 64 + 128 * j, 128 + 128 * j)
+
+    def win(buf, j, h, p=ALL):
+        a = 128 * j + 64 * (1 - h)
+        return cols(buf, a, a + 128, p=p)
+
+    for s_ in (0, 1):
+        v = cols("v16", 64 * s_, 64 * s_ + 64)
+        eq(blkw("wf", s_), v, q0, 1)
+        eq(blkw("wb", s_), v, q0, R); eq(blkw("wb", 2 + s_), v, q0, -32 * R); eq(blkw("wb", 4 + s_), v, q0, 0.5)
+        eq(cols("wf", 64 + 128 * (2 + s_), 128 + 128 * (2 + s_), p=p24), cols("vg", 64 * s_, 64 * s_ + 64, p=p24), ap("uf", p24, slice(1, 2)), 1)
+        eq(blkw("wb", 6 + s_), cols("vp", 64 * s_, 64 * s_ + 64), q0, 0.5)
+    eq(blkw("wf", 4), cols("vp", 0, 64), u63, 1)
+    if rolled[0]:
+        iota(cols("vj", 0, 64), [[-32, 2], [1, 32]], 32, 0)
+        eq(blkw("wf", 5), cols("vj", 0, 64), u63, 1)
+    for k in range(16):
+        eq(cols("pen", 128 * k, 128 * k + 128), ap("vb"), cols("uq", k, k + 1), -4)
+    sel(cols("rep", 0, 256), ap("one"), [[-64, 2], [0, 2], [-1, 64]], ALU.is_equal, 0.0, 0, 1)
+    if any(rolled):
+        sel(cols("rep", 256, 384), cols("one", 0, 128), [[-64, 2], [32, 2], [-1, 32]], ALU.is_equal, 0.0, -32, 1)
+    for j in range(nv // 64):
+        for h in (0, 1):
+            ts(cols("v3", 128 * j + 64 * h, 128 * j + 64 * h + 64, p=p24), cols("vg", 64 * j, 64 * j + 64, p=p24), 3.0, None, ALU.mult)
+        for l in range(3):
+            eq(cols("dsel", 128 * (3 * j + l), 128 * (3 * j + l + 1), p=p24), cols("v3", 128 * j, 128 * j + 128, p=p24),
+               ap("uq", p24, slice(l, l + 1)), 1)
+    iota(ap("rst"), [[0, HE], [256, NS]], 0, 0)
+    for h in (0, 1):
+        iota(ap("ec", slice(64 * h, 64 * h + 64), ALL), [[1, HE]], V + 2 * E + HE * h, 0)
+    cp(ap("dlb", p24, ALL), ap("dln", p24, ALL))
+    cp(ap("nxf"), ap("nxn"))
+    ts(ap("c3f", p24, ALL), ap("c3n", p24, ALL), ap("ab", p24, slice(0, 1)), ap("ab", p24, slice(4, 5)), ALU.mult, ALU.min)
+    p1 = slice(0, 1)
+    ones = cols("one", 0, HE, p=p1)
+    cp(ap("ffn"), ap("fdn"))
+    act(ap("ngn"), ap("ffn"), AF.Relu, scale=-1.0)
+    p2 = slice(0, 2)
+    mset(cols("cst", 256, 384, p=p2), R)
+    sel(cols("cst", 256, 384, p=p2), cols("cst", 256, 384, p=p2), [[0, 128]], ALU.is_gt, -1.0, 1, -1)
+    eq(ap("idk"), ap("vp"), q0, 1.0 / KF); eq(ap("prb"), ap("vp"), q0, R)
+
+    def tmp(s_, j):
+        return cols("ps%d" % (5 + s_), HE * j, HE * j + HE)
+
+    def half(buf, l, h, base=0, p=ALL):
+        a = base + E * l + HE * h
+        return cols(buf, a, a + HE, p=p)
+
+    def pack_rows(s_, l):
+        q = cols("q%d" % s_, HE * l, HE * l + HE)
+        if l == 0:
+            t = tmp(s_, 1)
+            mm([(t, win("wf", s_, h), half("ffn", l, h)) for h in (0, 1)] + [(t, win("wb", s_, h), half("pwn", l, h)) for h in (0, 1)]
+               + [(t, win("wb", 2 + s_, h), half("ngn", l, h)) for h in (0, 1)] + [(t, cols("cst", 0, 128, p=p1), ones)])
+            act(q, t, AF.Relu)
+        else:
+            t = cols("ps7", HE, E)
+            a = HE * (2 * s_ + l - 1)
+            kf = cols("kf", a, a + HE)
+            ts(kf, cols("fds", a, a + HE), 1.0, KF, ALU.add, ALU.mult)
+            mm([(t, ap("idk"), kf), (t, ap("prb"), cols("pws", a, a + HE)), (t, cols("cst", 256, 384, p=p2), cols("one", 0, HE, p=p2))])
+            tt(q, kf, t, ALU.min)
+
+    def base(rd, l, s_):
+        t = cols("ps7", 0, HE)
+        mm([(t, win("wb", 4 + s_, h), half("bsn", l, h)) for h in (0, 1)]
+           + [(t, win("wb", 6 + h, h), half("wa%d" % s_, l, h)) for h in (0, 1)] + [(t, cols("cst", 128, 256, p=p1), ones)])
+        b = slot("sl%d" % s_, NW)
+        ts(b, t, MAGIC, MAGIC, ALU.add, ALU.subtract)
+        mm([(cols("ps3", HE * s_, HE * s_ + HE), ap("ib"), b)])
+
+    def places(s_):
+        for l in range(3):
+            t = cols("ps7", 12 * l, 12 * l + 12)
+            mm([(t, win("wf", s_, h), cols("nxf", 24 * l + 12 * h, 24 * l + 12 * h + 12)) for h in (0, 1)])
+        cp(ap("nxo%d" % s_), cols("ps7", 0, 36))
+        mset(ap("sc%d" % s_), 0.0)
+
+    mb = [0]
+
+    def stage(rd, l, s_):
+        n = lambda x: ap("%s%d" % (x, s_))
+        wname = ("wa%d" if rd == 0 else "wc%d") % s_
+        q = cols("q%d" % s_, HE * l, HE * l + HE)
+        final = rd == 1 and l == 2
+        t0_, t1_ = tmp(s_, 0), tmp(s_, 1)
+        arr = None
+        qn = n("qn")
+        if QDMA:
+            qb = cols("qb%d" % s_, HE * l, HE * l + HE)
+            q, qn = (q, qb) if rd == 0 else (qb, qn)
+        act(n("en"), q, AF.Exp, bias=LNK, scale=-CL / R)
+        if rd == 1 and l == 0:
+            iq = n("iz"); arr = 2 + s_
+            act(n("ei"), iq, AF.Exp, bias=LNK + math.log(ALPHA), scale=-CL / R, arr=arr)
+        else:
+            iq = n("iq")
+            if l == 0:
+                mm([(t0_, win("wf", 2 + s_, h, p=p24), half("c3f", 0, h, p=p24)) for h in (0, 1)] + [(t0_, cols("cst", 0, 128, p=p1), ones)])
+                act(iq, t0_, AF.Relu)
+                act(n("ei"), iq, AF.Exp, bias=LNK + math.log(ALPHA), scale=-CL / R)
+            else:
+                mm([(t0_, win("wf", 4, h), half("sc%d" % s_, l - 1, h)) for h in (0, 1)])
+                act(n("ei"), t0_, AF.Exp, bias=LNK + math.log(ALPHA), scale=-CL / R)
+                act(iq, t0_, AF.Copy)
+        mm([(t1_, ap("tri"), n("en")), (t1_, ap("nib"), n("ei"))])
+        tt(t1_, iq, t1_, ALU.min, arr=arr)
+        tt(qn, q, t1_, ALU.max)
+        act(n("wn"), qn, AF.Identity, bias=128.0, scale=1.0 / R)
+        mm([(t0_, ap("idf"), qn), (t0_, ap("nrb"), n("wn"))])
+        ts(n("of"), t0_, 128 * R, None, ALU.add)
+        if not final:
+            mm([(t1_, ap("blk"), q), (t1_, ap("nblk"), qn), (t1_, ap("idf"), iq)], arr=arr)
+            act(n("hq"), t1_, AF.Copy)
+            act(n("eh"), n("hq"), AF.Exp, bias=K2 + math.log(ALPHA), scale=CL / R)
+        bp = cols("ps3", HE * s_, HE * s_ + HE)
+        tag[0] = 6 * rd + 2 * l + s_
+        w = HE // GCH
+        for j in range(GCH):
+            o = cols("ga%d" % s_, 16 * w * j, 16 * w * (j + 1))
+            src = ind(ap(wname), cols("of%d" % s_, w * j, w * j + w))
+            a_ = (s_ if rd == 0 else 2 + s_) if l == 0 else None
+            if (6 * rd + 2 * l + s_, j) in VGATHER:
+                cp(o, src, arr=a_)
+            else:
+                act(o, src, AF.Copy, arr=a_)
+        if rd == 0 and l < 2:
+            pack_rows(s_, l + 1)
+        cn = cols("ps4", 0, HE)
+        mm([(cn, ap("nib"), n("wn"))], last=False)
+        edges = [0, CSPLIT, HE] if CSPLIT else [0, HE]
+        for a, z in zip(edges, edges[1:]):
+            for k in range(16 if z == HE else NSPLIT):
+                a2 = a if k < NSPLIT else 0
+                c = cols("cmp", HE * k + a2, HE * k + z)
+                tt(c, cols("ga%d" % s_, 16 * a2 + k, 16 * z, 16), cols("ps3", HE * s_ + a2, HE * s_ + z), ALU.is_gt)
+                if z == HE:
+                    mm([(cn, cols("cwin", 15 - k, 143 - k), cols("cmp", HE * k, HE * k + HE))], first=False, last=(k == 15), acc=True)
+        ts(n("dr"), cn, -128.5, 64.0, ALU.is_gt, ALU.mult)
+        if not final:
+            mm([(t0_, ap("ib"), n("wn")), (t0_, ap("ib"), n("dr"))])
+            act(n("ed"), t0_, AF.Exp, bias=-192 * CL + K2, scale=CL)
+            mm([(t1_, ap("tri"), n("ed")), (t1_, ap("nib"), n("eh"))])
+            stay = rd == 0 and not QDMA
+            gq_ = q if stay else n("gn")
+            if NG_ACT:
+                act(t1_, t1_, AF.Relu, scale=-1.0 if stay else 1.0)
+                tt(gq_, qn, t1_, ALU.min)
+            else:
+                ts(t1_, t1_, 0.0, None, ALU.is_le if stay else ALU.is_gt)
+                tt(gq_, qn, t1_, ALU.mult)
+            mm([(t0_, ap("blk"), qn), (t0_, ap("nblk"), q)] if stay else [(t0_, ap("blk"), gq_)])
+            if rd == 0 and QDMA:
+                act(q, gq_, AF.Copy, scale=-1.0)
+                dma("G", [(qn, q)], 100e3, accum=True)
+            tt(n("ou"), n("hq"), t0_, ALU.max)
+            tgt = ind(cols("sc%d" % s_, E * l, E * l + E), cols("nxo%d" % s_, 12 * l, 12 * l + 12))
+            if l < 2:
+                cp(tgt, n("ou"))
+            else:
+                act(n("wo"), n("ou"), AF.Identity, bias=128.0, scale=1.0 / R)
+                act(n("rw"), n("wo"), AF.Identity, bias=-128 * R, scale=R)
+                tt(tgt, n("rw"), ap("ec"), ALU.add)
+                mm([(t1_, win("wf", 5 if rolled[0] else 4, h), half("sc%d" % s_, 2, h)) for h in (0, 1)])
+                act(n("isd"), t1_, AF.Copy)
+                remote([(0, n("isd"), n("iz"))], 2 + s_, 100e3)
+        for j in range(8):
+            bank = "ps%d" % (mb[0] % 3); mb[0] += 1
+            ks = (2 * j, 2 * j + 1)
+            outs = [cols(bank, i, E, 2) if PAIR else cols(bank, HE * i, HE * i + HE) for i in (0, 1)]
+            if 2 * j < NX:
+                for i in (0, 1):
+                    o = cols(bank, HE * i, HE * i + HE)
+                    mm([(o, cols("pen", 128 * ks[i], 128 * ks[i] + 128), n("dr"))])
+                for i in (0, 1):
+                    tt(slot("sl%d" % s_, ks[i]), cols("ga%d" % s_, ks[i], 3072, 16), cols(bank, HE * i, HE * i + HE), ALU.add)
+                continue
+            for i in (0, 1):
+                mm([(outs[i], ap("ib"), cols("ga%d" % s_, ks[i], 3072, 16)), (outs[i], cols("pen", 128 * ks[i], 128 * ks[i] + 128), n("dr"))])
+            for src, sj, m in ([(cols(bank, 0, E), 2 * j % NW, 2)] if PAIR else [(outs[i], ks[i] % NW, 1) for i in (0, 1)]):
+                d = slot("sl%d" % s_, sj, m)
+                if 2 * j < NW:
+                    act(d, src, AF.Copy)
+                else:
+                    tt(d, d, src, ALU.max)
+        add("V", [("tensor_tensor_scan", (n("so"), ap("rst"), n("sl"), 0.0, ALU.min, ALU.max), {})], [ap("rst"), n("sl")], [n("so")],
+            work(vi=1, cyc=0.5 * HE * NS))
+        m_ = slot("so%d" % s_, NW)
+        t = cols("ps7", 0, E)
+        j = 3 * s_ + l
+        mm([(t, cols("dsel", 128 * j, 128 * j + 128, p=p24), ap("dlb", p24, ALL))]
+           + [(cols("ps7", HE * h, HE * h + HE), cols("rep", 128 * h, 128 * h + 128), m_) for h in (0, 1)])
+        ts(cols(wname, E * l, E * l + E), t, 255.0, None, ALU.min)
+        if rd == 0 and any(rolled):
+            mm([(t, cols("rep", 256, 384), cols(wname, E * l, E * l + E))])
+            act(cols("rb%d" % s_, E * l, E * l + E), t, AF.Copy)
+        if not final:
+            base(rd + (l == 2), (l + 1) % 3, s_)
+        if rd == 0:
+            remote([(w_, cols(("rb%d" if rolled[w_] else "wa%d") % s_, E * l, E * l + E),
+                     cols("wc%d" % s_, V * (w_ + 1) + E * l, V * (w_ + 1) + E * l + E)) for w_ in (0, 1)], 2 + s_, 200e3)
+        else:
+            dma("S", [(ap("yt", slice(16 * gq, 16 * (gq + c), None), slice(E * l, E * l + E)),
+                       ap(wname, slice(16 * s, 16 * (s + c)), slice(E * l, E * l + E))) for s, gq, c in runs(s_, 0)], 50e3)
+
+    for s_ in (0, 1):
+        pack_rows(s_, 0)
+        base(0, 0, s_)
+    for s_ in (0, 1):
+        places(s_)
+    for rd in (0, 1):
+        for l in range(3):
+            for s_ in (0, 1):
+                tag[0] = max(0, 6 * rd + 2 * l + s_ - 2)
+                stage(rd, l, s_)
+    return ops, arr_total
+
+
+def schedule(ops):
+    n = len(ops)
+    hist = {}
+    sends = {}
+    for i, o in enumerate(ops):
+        deps = set()
+        for regs, is_w in ((o["rd"], False), (o["wr"], True)):
+            for r in regs:
+                for j, w, r2 in hist.get(r[0], ()):
+                    if (w or is_w) and r[1] < r2[2] and r2[1] < r[2] and r[3] & r2[3]:
+                        deps.add(j)
+        for r in o["wr"]:
+            hist[r[0]] = [x for x in hist.get(r[0], []) if not (r[1] <= x[2][1] and x[2][2] <= r[2] and (x[2][3] & ~r[3]) == 0)]
+        for r in o["wr"]:
+            hist[r[0]].append((i, True, r))
+        for r in o["rd"]:
+            hist.setdefault(r[0], []).append((i, False, r))
+        deps.discard(i)
+        o["deps"] = deps
+        o["soft"] = set(sends.get(o["arr"], ())) if o["arr"] is not None else set()
+        if o["kind"] == "r":
+            sends.setdefault(o["sends"], []).append(i)
+    succ = [[] for _ in ops]
+    left = [0] * n
+    for i, o in enumerate(ops):
+        for j in o["deps"] | o["soft"]:
+            succ[j].append(i); left[i] += 1
+    eng = [o["eng"] for o in ops]
+    banks = [sorted(o["banks"]) for o in ops]
+    pred = [[(k, not (o["acc"] and eng[k] == "P")) for k in sorted(o["deps"] | o["soft"])] for o in ops]
+    costs = [([float(o["cost"] @ w) for o in ops], [float(o["hold"] @ w) for o in ops], lat) for w, lat in RATES]
+
+    def place(boost, thr, frac, lead):
+        cost, hold, lat = costs[0]
+        prio = [0.0] * n
+        for i in range(n - 1, -1, -1):
+            prio[i] = cost[i] + lat + max([prio[j] for j in succ[i]], default=0.0)
+        prio = [p + boost[i] - lead * ops[i]["tag"] for i, p in enumerate(prio)]
+        free = dict.fromkeys("VAPGS", 0.0)
+        bank = {}
+        lf = list(left)
+        dep_t = [0.0] * n
+        end = [0.0] * n
+        extra = [()] * n
+        ready = [i for i in range(n) if lf[i] == 0]
+        order = []
+        while ready:
+            st = []
+            for i in ready:
+                t = max(free[eng[i]], dep_t[i])
+                for b in banks[i]:
+                    for e, j in bank.get(b, {}).items():
+                        if e != eng[i] and end[j] + lat > t:
+                            t = end[j] + lat
+                st.append((t, i))
+            t, i0 = min(st)
+            lim = t + thr + frac * hold[i0]
+            p, i, t = max((prio[i], -i, s) for s, i in st if eng[i] == eng[i0] and s <= lim)
+            i = -i
+            end[i] = t + cost[i]
+            free[eng[i]] = t + hold[i]
+            ex = []
+            for b in banks[i]:
+                ex += [j for e, j in bank.get(b, {}).items() if e != eng[i]]
+                bank.setdefault(b, {})[eng[i]] = i
+            extra[i] = ex
+            order.append(i); ready.remove(i)
+            for j in succ[i]:
+                lf[j] -= 1
+                if lf[j] == 0:
+                    dep_t[j] = max(end[k] + (lat if w else 0.0) for k, w in pred[j])
+                    ready.append(j)
+        return order, extra
+
+    def span(order, extra, m):
+        cost, hold, lat = costs[m]
+        free = dict.fromkeys("VAPGS", 0.0)
+        end = [0.0] * n
+        beg = [0.0] * n
+        for i in order:
+            t = free[eng[i]]
+            for k, w in pred[i]:
+                t = max(t, end[k] + (lat if w else 0.0))
+            for k in extra[i]:
+                t = max(t, end[k] + lat)
+            beg[i] = t
+            end[i] = t + cost[i]
+            free[eng[i]] = t + hold[i]
+        return max(end), beg
+
+    state = [12345]
+
+    def rnd():
+        state[0] = (state[0] * 1103515245 + 12345) % 2147483648
+        return state[0] / 2147483648.0
+
+    by = {}
+    for i, o in enumerate(ops):
+        name = o["wr"][0][0].rstrip("01") if o["wr"] else ""
+        by.setdefault((eng[i], name, -1), []).append(i)
+        by.setdefault((eng[i], name, o["tag"]), []).append(i)
+    kinds = [by[k] for k in sorted(by)]
+    best = None
+    boost = [0.0] * n
+    for k in range(TRIES):
+        if k < 60:
+            trial = (boost, 0.1 + 0.15 * (k % 2), 0.2 * (k // 2 % 3), 3.0 * (k // 6))
+        else:
+            b0, thr, frac, lead = best[3]
+            amp = 12 * rnd() * rnd()
+            b1 = list(b0)
+            if rnd() < 0.8:
+                pick = kinds[int(rnd() * len(kinds))]
+                dlt = amp * (rnd() - 0.5)
+                for i in pick:
+                    b1[i] += dlt
+            else:
+                for _ in range(1 + int(rnd() * 12)):
+                    b1[int(rnd() * n)] += amp * (rnd() - 0.5)
+            if rnd() < 0.15:
+                thr, frac = max(0.0, thr + 0.1 * (rnd() - 0.5)), min(1.0, max(0.0, frac + 0.3 * (rnd() - 0.5)))
+            trial = (b1, thr, frac, lead + (rnd() - 0.5 if rnd() < 0.1 else 0.0))
+        order, extra = place(*trial)
+        sp = [span(order, extra, m)[0] for m in range(len(RATES))]
+        score = sp[0] + 0.6 * sp[1] + 0.4 * sp[2]
+        if best is None or score < best[0]:
+            best = (score, order, extra, trial, sp)
+    beg = span(best[1], best[2], 0)[1]
+    for i, o in enumerate(ops):
+        o["deps"] |= set(best[2][i])
+        o["start"] = beg[i]; o["end"] = beg[i] + costs[0][0][i]; o["held"] = costs[0][1][i]
+    ops[0]["spans"] = best[4]
+    return best[1]
+
+
+def rank_program(g, core, T, topo):
+    rank = T.rank_of(core)
+    if rank is None:
+        return
+    ops, arr_total = build(rank, core, list(T.cores), topo)
+    order = schedule(ops)
+    queue = {"V": g.vector, "A": g.scalar, "P": g.tensor, "G": g, "S": g.sync}
+    method = {
+        "tensor_scalar": g.vector.tensor_scalar, "tensor_tensor": g.vector.tensor_tensor, "tensor_copy": g.vector.tensor_copy,
+        "memset": g.vector.memset, "tensor_tensor_scan": g.vector.tensor_tensor_scan, "activation": g.scalar.activation,
+        "matmul": g.tensor.matmul, "iota": g.iota, "affine_select": g.affine_select}
+
+    def real(a):
+        if isinstance(a, tuple) and a[0] == "ap":
+            return T[a[1]][a[2]]
+        if isinstance(a, tuple) and a[0] == "ind":
+            return real(a[1]).indirect(real(a[2]))
+        return a
+
+    needed = set()
+    for o in ops:
+        needed |= set(j for j in o["deps"] if not (o["acc"] and ops[j]["eng"] == "P"))
+    count = dict.fromkeys("VAPG", 0)
+    known = {e: {} for e in "VAPGS"}
+    totals = {}
+
+    def wait(e, sem, val):
+        if known[e].get(sem, 0) < val:
+            queue[e].wait_ge(T.sem[sem], val)
+            known[e][sem] = val
+
+    for i in order:
+        o = ops[i]; e = o["eng"]
+        need = {}
+        for j in o["deps"]:
+            if o["acc"] and ops[j]["eng"] == "P":
+                continue
+            sem, val = ops[j]["sig"]
+            need[sem] = max(need.get(sem, 0), val)
+        if e == "G" and o["kind"] == "c":
+            needed.add(i)
+            need["eG"] = count["G"]
+        if o["arr"] is not None:
+            need["arr%d" % o["arr"]] = arr_total[o["arr"]]
+        for sem in sorted(need):
+            wait(e, sem, need[sem])
+        if o["kind"] == "r":
+            tr = [RemoteDMATransfer(dst_ids=[DstId(rid=a[0], pnc=a[1])], dma_engine_mask=m, remote_sem=T.sem[o["rsem"]],
+                                    src=real(s), dst=real(d)) for a, m, s, d in o["calls"][0][1]]
+            g.remote_dma_fused(tr, local_sem=T.sem[o["sem"]])
+            o["sig"] = (o["sem"], o["total"])
+        elif o["kind"] == "d":
+            for _, args, _k in o["calls"]:
+                queue[e].dma_start(real(args[0]), real(args[1]), **_k).then_inc(T.sem[o["sem"]], 16)
+            o["sig"] = (o["sem"], o["total"])
+        else:
+            ins = None
+            for name, args, kw in o["calls"]:
+                ins = method[name](*[real(a) for a in args], **kw)
+            if i in needed:
+                count[e] += 1
+                ins.then_inc(T.sem["e" + e], 1)
+            o["sig"] = ("e" + e, count[e])
+        totals[o["sig"][0]] = max(totals.get(o["sig"][0], 0), o["sig"][1])
+    for k in range(4):
+        totals["arr%d" % k] = arr_total[k]
+    for sem in sorted(totals):
+        if totals[sem] > 0 and max(known[e].get(sem, 0) for e in known) < totals[sem]:
+            wait("S", sem, totals[sem])

@@ -13,16 +13,21 @@ LNK = 114 * math.log(2.0)
 MAGIC = 12582912.0
 PAIR = False
 NW = 8
-NS = NW + 1
+CAP = False
+B_ACT = False
+NS = NW + 1 + CAP
 GCH = 4
 NX = 0
 KF = 1048576.0
 K2 = 24 * math.log(2.0)
-NG_ACT = True
+NG_ACT = False
 QDMA = True
-VGATHER = {(0, 1), (0, 3)}
-TRIES = 600
-CSPLIT, NSPLIT = 96, 16
+VGATHER = {(0, 1), (0, 3), (11, 3), (10, 3), (6, 3), (7, 3)}
+BP16 = False
+WN_V, ED_V = True, True
+ORDER = [0, 1, 4, 2, 5, 3, 6, 7]
+TRIES = 700
+CSPLIT, NSPLIT = 96, 10
 
 SCRATCH = {
     "fdn": ("sbuf", [128, E], "int32"), "ffn": ("sbuf", [128, E], "float32"), "ngn": ("sbuf", [128, E], "bfloat16"),
@@ -44,15 +49,12 @@ SCRATCH = {
     "rep": ("sbuf", [128, 512], "bfloat16"), "dsel": ("sbuf", [128, 12 * 128], "bfloat16"),
     "ec": ("sbuf", [128, HE], "float32"), "cmp": ("sbuf", [128, 3072], "bfloat16"),
 }
-if PAIR:
-    SCRATCH["rst"] = ("sbuf", [128, HE, NS], "bfloat16")
-else:
-    SCRATCH["rst"] = ("sbuf", [128, HE * NS], "bfloat16")
 for _s in (0, 1):
+    SCRATCH["rst%d" % _s] = ("sbuf", [128, HE * NS], "bfloat16")
     for _n, _w, _d in (("wa", W3, "bfloat16"), ("wc", W3, "bfloat16"), ("rb", V, "bfloat16"), ("ga", 3072, "bfloat16"),
                        ("q", 3 * HE, "float32"), ("qn", HE, "float32"), ("qb", 3 * HE, "float32"), ("gn", HE, "float32"), ("iq", HE, "float32"), ("iz", HE, "float32"),
                        ("isd", HE, "float32"), ("en", HE, "bfloat16"), ("ei", HE, "bfloat16"), ("wn", HE, "bfloat16"),
-                       ("of", HE, "uint16"), ("hq", HE, "float32"), ("eh", HE, "bfloat16"), ("ed", HE, "bfloat16"),
+                       ("of", HE, "uint16"), ("hq", HE, "float32"), ("eh", HE, "bfloat16"), ("ed", HE, "bfloat16"), ("ep", HE, "bfloat16"),
                        ("dr", HE, "bfloat16"), ("ou", HE, "float32"), ("rw", HE, "float32"), ("wo", HE, "bfloat16"),
                        ("sc", 3 * E, "float32"), ("nxo", 36, "uint16")):
         SCRATCH["%s%d" % (_n, _s)] = ("sbuf", [128, _w], _d)
@@ -60,6 +62,9 @@ for _s in (0, 1):
         SCRATCH["%s%d" % (_n, _s)] = ("sbuf", [128, HE, NS] if PAIR else [128, HE * NS], "bfloat16")
 for _b in range(8):
     SCRATCH["ps%d" % _b] = ("psum", [128, 512], "float32")
+if BP16:
+    SCRATCH["ps3"] = ("psum", [128, 1024], "bfloat16")
+    SCRATCH["bt"] = ("sbuf", [128, 256], "bfloat16")
 SEMAPHORES = ["eV", "eA", "eP", "eG", "arr0", "arr1", "arr2", "arr3"] + ["d%d" % _i for _i in range(48)] + ["l%d" % _i for _i in range(12)]
 
 IO_SHAPES = {"fd": [128, V], "pw": [128, V], "bs": [128, V], "t0": [128, V], "yt": [128, V], "nx": [128, 72],
@@ -76,8 +81,8 @@ def rates(f, vi, ga, sc, pi, pe, lat):
     return np.array([1.0, vi, 0.00083 * f, 0.00083 * f * ga, 0.00083 * f * sc, pi, pe * f]), lat
 
 
-RATES = [rates(1.25, 0.04, 1.56, 3.8, 0.01, 0.00042, 0.1), rates(1.05, 0.02, 1.15, 2.2, 0.0, 0.00042, 0.06),
-         rates(1.4, 0.05, 1.95, 5.2, 0.01, 0.00042, 0.18)]
+RATES = [rates(1.1, 0.06, 1.56, 3.8, 0.015, 0.00042, 0.18), rates(1.0, 0.07, 1.15, 2.0, 0.01, 0.00052, 0.12),
+         rates(1.4, 0.05, 1.9, 5.0, 0.02, 0.00042, 0.2)]
 
 
 def ap(name, *idx):
@@ -182,10 +187,11 @@ def build(rank, core, cores, topo):
         c = work(vi=1.3, ga=nel(out)) if in_[0] == "ind" else work(vi=1.3, cyc=max(64, nel(out)))
         return add("A", [("activation", (out, in_, func), k)], [in_], [out], c, **kw)
 
-    def mm(terms, first=True, last=True, **kw):
+    def mm(terms, first=True, last=True, each=None, **kw):
         calls, c, rd, wr = [], 0.0, [], []
+        each = each or len(terms)
         for i, (out, l, r) in enumerate(terms):
-            calls.append(("matmul", (out, l, r, first and i == 0, last and i == len(terms) - 1), {}))
+            calls.append(("matmul", (out, l, r, first and i % each == 0, last and i % each == each - 1), {}))
             c = c + work(pi=1, pe=max(64, nel(r)) * (4 if SCRATCH[r[1]][2] == "float32" else 1))
             rd += [l, r]; wr.append(out)
         return add("P", calls, rd, wr, c, **kw)
@@ -226,7 +232,7 @@ def build(rank, core, cores, topo):
     def remote(items, arr, nbytes):
         s = "l%d" % nl[0]; nl[0] += 1
         tr = [(topo.addr(dests[w], core), my_masks[w], src, dst) for w, src, dst in items]
-        return add("G", [("remote", tr, {})], [x[1] for x in items], [], work(us=2.5 + nbytes / 60e3), hold=work(us=0.3), kind="r", sem=s,
+        return add("G", [("remote", tr, {})], [x[1] for x in items], [], work(us=2.5 + nbytes / 90e3), hold=work(us=0.3), kind="r", sem=s,
                    total=sum(my_n[w] for w, _, _ in items), rsem="arr%d" % arr, sends=arr)
 
     rolled = [(rank + 1) % 4 < rank, (rank + 2) % 4 < rank]
@@ -332,7 +338,11 @@ def build(rank, core, cores, topo):
         for l in range(3):
             eq(cols("dsel", 128 * (3 * j + l), 128 * (3 * j + l + 1), p=p24), cols("v3", 128 * j, 128 * j + 128, p=p24),
                ap("uq", p24, slice(l, l + 1)), 1)
-    iota(ap("rst"), [[0, HE], [256, NS]], 0, 0)
+    iota(ap("rst0"), [[0, HE], [256, NS]], 0, 0)["after"] = [i for i, o in enumerate(ops) if o["kind"] == "r"]
+    act(ap("rst1"), ap("rst0"), AF.Copy)
+    if CAP:
+        for s_ in (0, 1):
+            mset(slot("sl%d" % s_, NW + 1), 0.0)
     for h in (0, 1):
         iota(ap("ec", slice(64 * h, 64 * h + 64), ALL), [[1, HE]], V + 2 * E + HE * h, 0)
     cp(ap("dlb", p24, ALL), ap("dln", p24, ALL))
@@ -370,19 +380,50 @@ def build(rank, core, cores, topo):
             tt(q, kf, t, ALU.min)
 
     def base(rd, l, s_):
+        if BP16:
+            p96 = slice(0, 96)
+
+            def piece(buf, h, j):
+                a = E * l + HE * h + 96 * j
+                return cols(buf, a, a + 96)
+
+            terms = []
+            for j in (0, 1):
+                t = cols("ps7", 128 * j, 128 * j + 128, p=p96)
+                terms += ([(t, piece("bsn", h, j), win("wb", 4 + s_, h)) for h in (0, 1)]
+                          + [(t, piece("wa%d" % s_, h, j), win("wb", 6 + h, h)) for h in (0, 1)]
+                          + [(t, cols("one", 0, 96, p=p1), cols("cst", 128, 256, p=p1))])
+            mm(terms, each=5)
+            bt = ap("bt", p96, ALL)
+            ts(bt, cols("ps7", 0, 256, p=p96), MAGIC, MAGIC, ALU.add, ALU.subtract)
+            outs = [cols("ps3", HE * s_ + 96 * j, HE * s_ + 96 * j + 96) for j in (0, 1)]
+            add("P", [("transpose", (outs[j], cols("bt", 128 * j, 128 * j + 128, p=p96), cols("ib", 0, 96, p=p96)), {}) for j in (0, 1)],
+                [bt, ap("ib")], outs, work(pi=2, pe=256))
+            act(slot("sl%d" % s_, NW), cols("ps3", HE * s_, HE * s_ + HE), AF.Copy)
+            return
         t = cols("ps7", 0, HE)
         mm([(t, win("wb", 4 + s_, h), half("bsn", l, h)) for h in (0, 1)]
            + [(t, win("wb", 6 + h, h), half("wa%d" % s_, l, h)) for h in (0, 1)] + [(t, cols("cst", 128, 256, p=p1), ones)])
         b = slot("sl%d" % s_, NW)
-        ts(b, t, MAGIC, MAGIC, ALU.add, ALU.subtract)
+        if B_ACT:
+            act(t, t, AF.Identity, bias=MAGIC)
+            act(b, t, AF.Identity, bias=-MAGIC)
+        else:
+            ts(b, t, MAGIC, MAGIC, ALU.add, ALU.subtract)
         mm([(cols("ps3", HE * s_, HE * s_ + HE), ap("ib"), b)])
+        if CAP:
+            j = 3 * s_ + l
+            mm([(cols("ps7", 0, E), cols("dsel", 128 * j, 128 * j + 128, p=p24), ap("dlb", p24, ALL))])
+            for h in (0, 1):
+                ph = slice(64 * h, 64 * h + 64)
+                act(cols("rst%d" % s_, NW + 1, HE * NS, NS, p=ph), cols("ps7", HE * h, HE * h + HE, p=ph), AF.Identity, bias=255.0, scale=-1.0)
 
     def places(s_):
         for l in range(3):
             t = cols("ps7", 12 * l, 12 * l + 12)
             mm([(t, win("wf", s_, h), cols("nxf", 24 * l + 12 * h, 24 * l + 12 * h + 12)) for h in (0, 1)])
         cp(ap("nxo%d" % s_), cols("ps7", 0, 36))
-        mset(ap("sc%d" % s_), 0.0)
+        act(ap("sc%d" % s_), ap("bsn"), AF.Identity, scale=0.0)
 
     mb = [0]
 
@@ -414,11 +455,16 @@ def build(rank, core, cores, topo):
         mm([(t1_, ap("tri"), n("en")), (t1_, ap("nib"), n("ei"))])
         tt(t1_, iq, t1_, ALU.min, arr=arr)
         tt(qn, q, t1_, ALU.max)
-        act(n("wn"), qn, AF.Identity, bias=128.0, scale=1.0 / R)
+        if WN_V:
+            ts(n("wn"), qn, 1.0 / R, 128.0, ALU.mult, ALU.add)
+        else:
+            act(n("wn"), qn, AF.Identity, bias=128.0, scale=1.0 / R)
+        if ED_V and not final:
+            act(n("ep"), n("wn"), AF.Exp, bias=-128 * CL + K2 - math.log(64.0), scale=CL)
         mm([(t0_, ap("idf"), qn), (t0_, ap("nrb"), n("wn"))])
         ts(n("of"), t0_, 128 * R, None, ALU.add)
         if not final:
-            mm([(t1_, ap("blk"), q), (t1_, ap("nblk"), qn), (t1_, ap("idf"), iq)], arr=arr)
+            mm([(t1_, ap("blk"), q), (t1_, ap("nblk"), qn), (t1_, ap("idf"), iq)], arr=arr, after=[len(ops) - 1])
             act(n("hq"), t1_, AF.Copy)
             act(n("eh"), n("hq"), AF.Exp, bias=K2 + math.log(ALPHA), scale=CL / R)
         bp = cols("ps3", HE * s_, HE * s_ + HE)
@@ -446,8 +492,12 @@ def build(rank, core, cores, topo):
                     mm([(cn, cols("cwin", 15 - k, 143 - k), cols("cmp", HE * k, HE * k + HE))], first=False, last=(k == 15), acc=True)
         ts(n("dr"), cn, -128.5, 64.0, ALU.is_gt, ALU.mult)
         if not final:
-            mm([(t0_, ap("ib"), n("wn")), (t0_, ap("ib"), n("dr"))])
-            act(n("ed"), t0_, AF.Exp, bias=-192 * CL + K2, scale=CL)
+            if ED_V:
+                mm([(t0_, ap("ib"), n("ep"))])
+                tt(n("ed"), n("dr"), t0_, ALU.mult)
+            else:
+                mm([(t0_, ap("ib"), n("wn")), (t0_, ap("ib"), n("dr"))])
+                act(n("ed"), t0_, AF.Exp, bias=-192 * CL + K2, scale=CL)
             mm([(t1_, ap("tri"), n("ed")), (t1_, ap("nib"), n("eh"))])
             stay = rd == 0 and not QDMA
             gq_ = q if stay else n("gn")
@@ -472,7 +522,7 @@ def build(rank, core, cores, topo):
                 mm([(t1_, win("wf", 5 if rolled[0] else 4, h), half("sc%d" % s_, 2, h)) for h in (0, 1)])
                 act(n("isd"), t1_, AF.Copy)
                 remote([(0, n("isd"), n("iz"))], 2 + s_, 100e3)
-        for j in range(8):
+        for j in ORDER:
             bank = "ps%d" % (mb[0] % 3); mb[0] += 1
             ks = (2 * j, 2 * j + 1)
             outs = [cols(bank, i, E, 2) if PAIR else cols(bank, HE * i, HE * i + HE) for i in (0, 1)]
@@ -483,22 +533,25 @@ def build(rank, core, cores, topo):
                 for i in (0, 1):
                     tt(slot("sl%d" % s_, ks[i]), cols("ga%d" % s_, ks[i], 3072, 16), cols(bank, HE * i, HE * i + HE), ALU.add)
                 continue
-            for i in (0, 1):
-                mm([(outs[i], ap("ib"), cols("ga%d" % s_, ks[i], 3072, 16)), (outs[i], cols("pen", 128 * ks[i], 128 * ks[i] + 128), n("dr"))])
+            mm([x for i in (0, 1) for x in ((outs[i], ap("ib"), cols("ga%d" % s_, ks[i], 3072, 16)),
+                                            (outs[i], cols("pen", 128 * ks[i], 128 * ks[i] + 128), n("dr")))], each=2)
             for src, sj, m in ([(cols(bank, 0, E), 2 * j % NW, 2)] if PAIR else [(outs[i], ks[i] % NW, 1) for i in (0, 1)]):
                 d = slot("sl%d" % s_, sj, m)
                 if 2 * j < NW:
                     act(d, src, AF.Copy)
                 else:
                     tt(d, d, src, ALU.max)
-        add("V", [("tensor_tensor_scan", (n("so"), ap("rst"), n("sl"), 0.0, ALU.min, ALU.max), {})], [ap("rst"), n("sl")], [n("so")],
+        add("V", [("tensor_tensor_scan", (n("so"), n("rst"), n("sl"), 0.0, ALU.min, ALU.max), {})], [n("rst"), n("sl")], [n("so")],
             work(vi=1, cyc=0.5 * HE * NS))
-        m_ = slot("so%d" % s_, NW)
+        m_ = slot("so%d" % s_, NS - 1)
         t = cols("ps7", 0, E)
         j = 3 * s_ + l
         mm([(t, cols("dsel", 128 * j, 128 * j + 128, p=p24), ap("dlb", p24, ALL))]
            + [(cols("ps7", HE * h, HE * h + HE), cols("rep", 128 * h, 128 * h + 128), m_) for h in (0, 1)])
-        ts(cols(wname, E * l, E * l + E), t, 255.0, None, ALU.min)
+        if CAP:
+            act(cols(wname, E * l, E * l + E), t, AF.Copy)
+        else:
+            ts(cols(wname, E * l, E * l + E), t, 255.0, None, ALU.min)
         if rd == 0 and any(rolled):
             mm([(t, cols("rep", 256, 384), cols(wname, E * l, E * l + E))])
             act(cols("rb%d" % s_, E * l, E * l + E), t, AF.Copy)
@@ -524,6 +577,9 @@ def build(rank, core, cores, topo):
     return ops, arr_total
 
 
+START = [{}, 0.08, 0.06, 10.0]
+
+
 def schedule(ops):
     n = len(ops)
     hist = {}
@@ -544,6 +600,7 @@ def schedule(ops):
         deps.discard(i)
         o["deps"] = deps
         o["soft"] = set(sends.get(o["arr"], ())) if o["arr"] is not None else set()
+        o["soft"] |= set(o.get("after", ()))
         if o["kind"] == "r":
             sends.setdefault(o["sends"], []).append(i)
     succ = [[] for _ in ops]
@@ -625,32 +682,32 @@ def schedule(ops):
         name = o["wr"][0][0].rstrip("01") if o["wr"] else ""
         by.setdefault((eng[i], name, -1), []).append(i)
         by.setdefault((eng[i], name, o["tag"]), []).append(i)
-    kinds = [by[k] for k in sorted(by)]
+    kinds = sorted(by)
+    wide = [k for k in kinds if k[2] == -1]
     best = None
-    boost = [0.0] * n
-    for k in range(TRIES):
-        if k < 60:
-            trial = (boost, 0.1 + 0.15 * (k % 2), 0.2 * (k // 2 % 3), 3.0 * (k // 6))
+    for k in range(TRIES if START[0] else int(2.5 * TRIES)):
+        if k == 0:
+            trial = (dict(START[0]),) + tuple(START[1:])
         else:
             b0, thr, frac, lead = best[3]
-            amp = 12 * rnd() * rnd()
-            b1 = list(b0)
-            if rnd() < 0.8:
-                pick = kinds[int(rnd() * len(kinds))]
-                dlt = amp * (rnd() - 0.5)
-                for i in pick:
-                    b1[i] += dlt
-            else:
-                for _ in range(1 + int(rnd() * 12)):
-                    b1[int(rnd() * n)] += amp * (rnd() - 0.5)
-            if rnd() < 0.15:
-                thr, frac = max(0.0, thr + 0.1 * (rnd() - 0.5)), min(1.0, max(0.0, frac + 0.3 * (rnd() - 0.5)))
-            trial = (b1, thr, frac, lead + (rnd() - 0.5 if rnd() < 0.1 else 0.0))
-        order, extra = place(*trial)
+            b1 = dict(b0)
+            for _ in range(1 + int(2 * rnd())):
+                pool = wide if rnd() < 0.3 else kinds
+                pick = pool[int(rnd() * len(pool))]
+                b1[pick] = round(b1.get(pick, 0.0) + 16 * rnd() * (rnd() - 0.5), 1)
+            if rnd() < 0.1:
+                thr, frac = max(0.0, round(thr + 0.1 * (rnd() - 0.5), 2)), min(1.0, max(0.0, round(frac + 0.3 * (rnd() - 0.5), 2)))
+            trial = (b1, thr, frac, round(lead + (4 * rnd() - 2 if rnd() < 0.1 else 0.0), 1))
+        boost = [0.0] * n
+        for key, x in trial[0].items():
+            for i in by.get(key, ()):
+                boost[i] += x
+        order, extra = place(boost, *trial[1:])
         sp = [span(order, extra, m)[0] for m in range(len(RATES))]
         score = sp[0] + 0.6 * sp[1] + 0.4 * sp[2]
-        if best is None or score < best[0]:
+        if best is None or score <= best[0]:
             best = (score, order, extra, trial, sp)
+    START[:] = best[3]
     beg = span(best[1], best[2], 0)[1]
     for i, o in enumerate(ops):
         o["deps"] |= set(best[2][i])
@@ -669,7 +726,7 @@ def rank_program(g, core, T, topo):
     method = {
         "tensor_scalar": g.vector.tensor_scalar, "tensor_tensor": g.vector.tensor_tensor, "tensor_copy": g.vector.tensor_copy,
         "memset": g.vector.memset, "tensor_tensor_scan": g.vector.tensor_tensor_scan, "activation": g.scalar.activation,
-        "matmul": g.tensor.matmul, "iota": g.iota, "affine_select": g.affine_select}
+        "matmul": g.tensor.matmul, "transpose": g.tensor.transpose, "iota": g.iota, "affine_select": g.affine_select}
 
     def real(a):
         if isinstance(a, tuple) and a[0] == "ap":

import math
import numpy as np
from concourse.bass import DstId, RemoteDMATransfer
from concourse.mybir import AluOpType, ActivationFunctionType

ALU = AluOpType
AF = ActivationFunctionType
E, HE, V, W3 = 384, 192, 1152, 3456
R = 57344.0
BETA, ALPHA = 40.0, 1.5
CL = math.log(BETA)
LNK = 114 * math.log(2.0)
MAGIC = 12582912.0
PAIR = False
NW = 8
CAP = False
B_ACT = False
NS = NW + 1 + CAP
GCH = 4
NX = 0
KF = 1048576.0
K2 = 24 * math.log(2.0)
NG_ACT = False
QDMA = True
VGATHER = {(0, 1), (0, 3), (11, 3), (10, 3), (6, 3), (7, 3)}
BP16 = False
WN_V, ED_V = True, True
ORDER = [0, 1, 4, 2, 5, 3, 6, 7]
TRIES = 700
CSPLIT, NSPLIT = 96, 10

SCRATCH = {
    "fdn": ("sbuf", [128, E], "int32"), "ffn": ("sbuf", [128, E], "float32"), "ngn": ("sbuf", [128, E], "bfloat16"),
    "pwn": ("sbuf", [128, E], "bfloat16"), "bsn": ("sbuf", [128, V], "bfloat16"),
    "fds": ("sbuf", [128, 4 * HE], "int32"), "pws": ("sbuf", [128, 4 * HE], "bfloat16"), "kf": ("sbuf", [128, 4 * HE], "float32"),
    "idk": ("sbuf", [128, 128], "float32"), "prb": ("sbuf", [128, 128], "bfloat16"),
    "nxn": ("sbuf", [128, 72], "int32"), "nxf": ("sbuf", [128, 72], "float32"),
    "dln": ("sbuf", [128, E], "int32"), "dlb": ("sbuf", [128, E], "bfloat16"),
    "c3n": ("sbuf", [128, E], "int32"), "c3f": ("sbuf", [128, E], "float32"), "ab": ("sbuf", [128, 8], "float32"),
    "one": ("sbuf", [128, 256], "bfloat16"), "cst": ("sbuf", [128, 384], "bfloat16"),
    "ui": ("sbuf", [128, 8], "int32"), "uf": ("sbuf", [128, 8], "float32"), "uq": ("sbuf", [128, 16], "float32"),
    "vp": ("sbuf", [128, 128], "bfloat16"), "vb": ("sbuf", [128, 128], "bfloat16"), "vj": ("sbuf", [128, 128], "bfloat16"),
    "v16": ("sbuf", [128, 256], "int32"), "vg": ("sbuf", [128, 256], "int32"), "v3": ("sbuf", [128, 512], "bfloat16"),
    "ib": ("sbuf", [128, 128], "bfloat16"), "nib": ("sbuf", [128, 128], "bfloat16"), "nrb": ("sbuf", [128, 128], "bfloat16"),
    "idf": ("sbuf", [128, 128], "float32"), "blk": ("sbuf", [128, 128], "float32"), "nblk": ("sbuf", [128, 128], "float32"),
    "tt1": ("sbuf", [128, 128], "float32"), "tt2": ("sbuf", [128, 128], "float32"), "tri": ("sbuf", [128, 128], "bfloat16"),
    "cwin": ("sbuf", [128, 144], "bfloat16"), "pen": ("sbuf", [128, 2048], "bfloat16"),
    "wb": ("sbuf", [128, 17 * 64], "bfloat16"), "wf": ("sbuf", [128, 13 * 64], "float32"),
    "rep": ("sbuf", [128, 512], "bfloat16"), "dsel": ("sbuf", [128, 12 * 128], "bfloat16"),
    "ec": ("sbuf", [128, HE], "float32"), "cmp": ("sbuf", [128, 3072], "bfloat16"),
}
for _s in (0, 1):
    SCRATCH["rst%d" % _s] = ("sbuf", [128, HE * NS], "bfloat16")
    for _n, _w, _d in (("wa", W3, "bfloat16"), ("wc", W3, "bfloat16"), ("rb", V, "bfloat16"), ("ga", 3072, "bfloat16"),
                       ("q", 3 * HE, "float32"), ("qn", HE, "float32"), ("qb", 3 * HE, "float32"), ("gn", HE, "float32"), ("iq", HE, "float32"), ("iz", HE, "float32"),
                       ("isd", HE, "float32"), ("en", HE, "bfloat16"), ("ei", HE, "bfloat16"), ("wn", HE, "bfloat16"),
                       ("of", HE, "uint16"), ("hq", HE, "float32"), ("eh", HE, "bfloat16"), ("ed", HE, "bfloat16"), ("ep", HE, "bfloat16"),
                       ("dr", HE, "bfloat16"), ("ou", HE, "float32"), ("rw", HE, "float32"), ("wo", HE, "bfloat16"),
                       ("sc", 3 * E, "float32"), ("nxo", 36, "uint16")):
        SCRATCH["%s%d" % (_n, _s)] = ("sbuf", [128, _w], _d)
    for _n in ("sl", "so"):
        SCRATCH["%s%d" % (_n, _s)] = ("sbuf", [128, HE, NS] if PAIR else [128, HE * NS], "bfloat16")
for _b in range(8):
    SCRATCH["ps%d" % _b] = ("psum", [128, 512], "float32")
if BP16:
    SCRATCH["ps3"] = ("psum", [128, 1024], "bfloat16")
    SCRATCH["bt"] = ("sbuf", [128, 256], "bfloat16")
SEMAPHORES = ["eV", "eA", "eP", "eG", "arr0", "arr1", "arr2", "arr3"] + ["d%d" % _i for _i in range(48)] + ["l%d" % _i for _i in range(12)]

IO_SHAPES = {"fd": [128, V], "pw": [128, V], "bs": [128, V], "t0": [128, V], "yt": [128, V], "nx": [128, 72],
             "dl": [8, V], "cf": [8, E], "cw": [8, E]}
WIDTH = {"float32": 4, "int32": 4, "bfloat16": 2, "uint16": 2}
ALL = slice(None)


def work(us=0.0, vi=0.0, cyc=0.0, ga=0.0, sc=0.0, pi=0.0, pe=0.0):
    return np.array([us, vi, cyc, ga, sc, pi, pe])


def rates(f, vi, ga, sc, pi, pe, lat):
    return np.array([1.0, vi, 0.00083 * f, 0.00083 * f * ga, 0.00083 * f * sc, pi, pe * f]), lat


RATES = [rates(1.1, 0.06, 1.56, 3.8, 0.015, 0.00042, 0.18), rates(1.0, 0.07, 1.15, 2.0, 0.01, 0.00052, 0.12),
         rates(1.4, 0.05, 1.9, 5.0, 0.02, 0.00042, 0.2)]


def ap(name, *idx):
    return ("ap", name, tuple(idx) if idx else (ALL,))


def cols(name, a, b, step=None, p=ALL):
    return ap(name, p, slice(a, b, step))


def ind(win, off):
    return ("ind", win, off)


def slot(name, j, n=1):
    if PAIR:
        return ap(name, ALL, ALL, slice(j, j + n)) if n > 1 else ap(name, ALL, ALL, j)
    return cols(name, j, HE * NS, NS)


_REG = {}


def region(a):
    key = repr(a)
    if key not in _REG:
        name, idx = a[1], a[2]
        shape = SCRATCH[name][1] if name in SCRATCH else IO_SHAPES[name]
        p = range(shape[0])[idx[0]]
        c = np.arange(int(np.prod(shape[1:]))).reshape(shape[1:])[idx[1:]].ravel()
        m = 0
        for x in c.tolist():
            m |= 1 << x
        _REG[key] = (name, p[0], p[-1] + 1, m, len(c))
    return _REG[key]


def two_bytes(aps):
    return all(WIDTH[SCRATCH[a[1]][2]] == 2 for a in aps)


def in_psum(a):
    return a[1].startswith("ps")


def build(rank, core, cores, topo):
    ops = []
    tag = [0]

    def add(eng, calls, reads, writes, cost, **kw):
        rd = []
        for a in reads:
            rd += [a[1], a[2]] if a[0] == "ind" else [a]
        wr = []
        for a in writes:
            if a[0] == "ind":
                wr.append(a[1]); rd.append(a[2])
            else:
                wr.append(a)
        o = dict(eng=eng, calls=calls, rd=[region(a) for a in rd], wr=[region(a) for a in wr], cost=cost, hold=cost,
                 kind="c", arr=None, acc=False, tag=tag[0])
        o.update(kw)
        o["banks"] = set(x[0] for x in o["rd"] + o["wr"] if x[0].startswith("ps"))
        ops.append(o)
        return o

    def nel(a):
        return 16 * region(a[2])[4] if a[0] == "ind" else region(a)[4]

    def aps(*xs):
        return [x for x in xs if isinstance(x, tuple)]

    def vcost(out, ins, f=1.0):
        if out[0] == "ind":
            return work(vi=1, sc=nel(out))
        if ins[0][0] == "ind":
            return work(vi=1, ga=nel(out))
        return work(vi=1, cyc=max(64, nel(out) * f))

    def ts(out, in0, s1, s2, op0, op1=None, **kw):
        args = (out, in0, s1, s2, op0) + ((op1,) if op1 is not None else ())
        f = 0.5 if in0[0] == "ap" and out[0] == "ap" and two_bytes([out, in0]) else 1.0
        return add("V", [("tensor_scalar", args, {})], aps(in0, s1, s2), [out], vcost(out, [in0], f), **kw)

    def tt(out, in0, in1, op, **kw):
        f = 1.0 if in0[0] == "ind" or in_psum(in0) or in_psum(in1) else 2.0
        return add("V", [("tensor_tensor", (out, in0, in1, op), {})], [in0, in1], [out], vcost(out, [in0], f), **kw)

    def cp(out, in_, **kw):
        f = 0.5 if in_[0] == "ap" and out[0] == "ap" and two_bytes([out, in_]) else 1.0
        return add("V", [("tensor_copy", (out, in_), {})], [in_], [out], vcost(out, [in_], f), **kw)

    def mset(out, c):
        return add("V", [("memset", (out, c), {})], [], [out], work(vi=1, cyc=max(64, nel(out) * (0.5 if two_bytes([out]) else 1.0))))

    def act(out, in_, func, bias=None, scale=None, **kw):
        k = {}
        if bias is not None:
            k["bias"] = float(bias)
        if scale is not None:
            k["scale"] = float(scale)
        c = work(vi=1.3, ga=nel(out)) if in_[0] == "ind" else work(vi=1.3, cyc=max(64, nel(out)))
        return add("A", [("activation", (out, in_, func), k)], [in_], [out], c, **kw)

    def mm(terms, first=True, last=True, each=None, **kw):
        calls, c, rd, wr = [], 0.0, [], []
        each = each or len(terms)
        for i, (out, l, r) in enumerate(terms):
            calls.append(("matmul", (out, l, r, first and i % each == 0, last and i % each == each - 1), {}))
            c = c + work(pi=1, pe=max(64, nel(r)) * (4 if SCRATCH[r[1]][2] == "float32" else 1))
            rd += [l, r]; wr.append(out)
        return add("P", calls, rd, wr, c, **kw)

    def iota(out, pattern, base, cm):
        k = {} if SCRATCH[out[1]][2] == "int32" else {"allow_small_or_imprecise_dtypes": True}
        return add("G", [("iota", (out, pattern, base, cm), k)], [], [out], work(us=0.15, cyc=2 * nel(out)))

    def sel(out, in_, pattern, op, fill, base, cm):
        return add("G", [("affine_select", (out, in_, pattern, op, fill, base, cm), {})], [in_], [out], work(us=0.2, cyc=2 * nel(out)))

    nd = [0]

    def dma(eng, pairs, nbytes, accum=False):
        s = "d%d" % nd[0]; nd[0] += 1
        calls = [("dma_start", (o, i), {"accum_op": ALU.add} if accum else {}) for o, i in pairs]
        return add(eng, calls, [i for o, i in pairs], [o for o, i in pairs], work(us=0.1 * len(pairs) + 1.9 + nbytes / 150e3),
                   hold=work(us=(1.0 if eng == "G" else 0.1) * len(pairs)), kind="d", sem=s, total=16 * len(pairs))

    dests = [cores[(rank + 1) % 4], cores[(rank + 2) % 4]]

    def masks(src, ds):
        lists = [topo.engines(src, d) for d in ds]
        if len(ds) == 2 and len(lists[0]) == len(lists[1]):
            h = len(lists[0]) // 2
            lists = [lists[0][:h], lists[1][h:]]
        elif len(ds) == 2:
            big = 0 if len(lists[0]) > len(lists[1]) else 1
            lists[big] = [e for e in lists[big] if e not in lists[1 - big]]
        return [sum(1 << e for e in x) for x in lists], [len(x) for x in lists]

    my_masks, my_n = masks(core, dests)
    from1 = masks(cores[(rank - 1) % 4], [core, cores[(rank + 1) % 4]])[1][0]
    from2 = masks(cores[(rank - 2) % 4], [cores[(rank - 1) % 4], core])[1][1]
    arr_total = {0: from1 + from2, 1: from1 + from2, 2: 4 * from1 + 3 * from2, 3: 4 * from1 + 3 * from2}
    nl = [0]

    def remote(items, arr, nbytes):
        s = "l%d" % nl[0]; nl[0] += 1
        tr = [(topo.addr(dests[w], core), my_masks[w], src, dst) for w, src, dst in items]
        return add("G", [("remote", tr, {})], [x[1] for x in items], [], work(us=2.5 + nbytes / 90e3), hold=work(us=0.3), kind="r", sem=s,
                   total=sum(my_n[w] for w, _, _ in items), rsem="arr%d" % arr, sends=arr)

    rolled = [(rank + 1) % 4 < rank, (rank + 2) % 4 < rank]

    def grp(s_, s):
        return (2 * s_ + (s & 1) + 4 * (s >> 1) + rank) % 8

    def runs(s_, x):
        out = []
        for s in range(4):
            gq = grp(s_, s ^ x)
            if out and out[-1][1] + out[-1][2] == gq and s % 2 == 1:
                out[-1][2] += 1
            else:
                out.append([s, gq, 1])
        return out

    def t0_pairs(buf, s_, x):
        return [(ap(buf, slice(64 * h + 16 * s, 64 * h + 16 * (s + n)), slice(0, V)), ap("t0", slice(16 * gq, 16 * (gq + n)), ALL))
                for h in (0, 1) for s, gq, n in runs(s_, x)]

    for s_ in (0, 1):
        if any(rolled):
            dma("S" if s_ == 0 else "A", t0_pairs("rb%d" % s_, s_, 2), 295e3)
        dma("A" if s_ == 0 else "S", t0_pairs("wa%d" % s_, s_, 0), 295e3)
        if s_ == 0:
            dma("S", [(cols("fdn", 0, E), cols("fd", 0, E))], 200e3)
            dma("A", [(cols("pwn", 0, E), cols("pw", 0, E))], 100e3)
            dma("S", [(ap("c3n", slice(0, 8), ALL), ap("cf")), (ap("c3n", slice(8, 16), ALL), ap("cw")),
                      (ap("c3n", slice(16, 24), ALL), ap("cf"))], 40e3)
        remote([(w, cols(("rb%d" if rolled[w] else "wa%d") % s_, 0, V), cols("wa%d" % s_, V * (w + 1), V * (w + 2))) for w in (0, 1)],
               s_, 590e3)
    dma("S", [(ap("bsn"), ap("bs"))], 295e3)
    dma("S", [(ap("nxn"), ap("nx")), (ap("dln", slice(0, 24), ALL), ap("dl"))], 80e3)
    for l in (1, 2):
        for s_ in (0, 1):
            a = HE * (2 * s_ + l - 1)
            dma("S", [(ap(buf, slice(64 * h + 16 * s, 64 * h + 16 * (s + c)), slice(a, a + HE)),
                       ap(src, slice(16 * gq, 16 * (gq + c)), slice(E * l + HE * h, E * l + HE * h + HE)))
                      for buf, src in (("fds", "fd"), ("pws", "pw")) for h in (0, 1) for s, gq, c in runs(s_, 0)], 150e3)
    for s_ in (0, 1):
        dma("S", t0_pairs("wc%d" % s_, s_, 0), 295e3)

    mset(ap("one"), 1.0)
    mset(cols("cst", 0, 128), R); mset(cols("cst", 128, 256), -0.25)
    mset(ap("wf"), 0.0); mset(ap("wb"), 0.0); mset(ap("cwin"), 0.0)
    mset(cols("ab", 0, 1), 1.0); mset(cols("ab", 4, 5), 1e9)
    iota(ap("uq"), [[-1, 16]], 0, 1)
    iota(cols("ui", 0, 1), [[0, 1]], 0, 1)
    iota(ap("vp"), [[1, 128]], 0, 0)
    iota(ap("vb"), [[16, 8], [0, 16]], 0, 0)
    for s_ in (0, 1):
        iota(cols("v16", 64 * s_, 64 * s_ + 64), [[64, 2], [16, 2], [1, 16]], 16 * (2 * s_ + rank), 0)
    nv = 128
    p24 = slice(0, 24)
    sel(ap("ab", p24, slice(0, 1)), ap("ab", p24, slice(0, 1)), [[0, 1]], ALU.is_gt, R, 8, -1)
    sel(ap("ab", p24, slice(0, 1)), ap("ab", p24, slice(0, 1)), [[0, 1]], ALU.is_gt, 32 * R, 16, -1)
    sel(ap("ab", p24, slice(4, 5)), ap("ab", p24, slice(4, 5)), [[0, 1]], ALU.is_gt, 0.0, 16, -1)
    for j, m in ((1, 7), (2, 63), (3, 112)):
        ts(cols("ui", j, j + 1), cols("ui", 0, 1), m, None, ALU.bitwise_and)
    cp(cols("uf", 0, 4), cols("ui", 0, 4))
    q0, u7, u63, u112 = cols("uq", 0, 1), cols("uf", 1, 2), cols("uf", 2, 3), cols("uf", 3, 4)

    def eq(out, row, col, c):
        return ts(out, row, col, float(c), ALU.is_equal, ALU.mult)

    eq(ap("ib"), ap("vp"), q0, 1); eq(ap("nib"), ap("vp"), q0, -1); eq(ap("nrb"), ap("vp"), q0, -R); eq(ap("idf"), ap("vp"), q0, 1)
    eq(ap("blk"), ap("vb"), u112, 1); eq(ap("nblk"), ap("vb"), u112, -1)
    eq(cols("cwin", 15, 143, 16), cols("vb", 0, 128, 16), u112, 1)
    c1, c2 = -ALPHA + ALPHA / BETA, -ALPHA / BETA
    ts(ap("tt1"), ap("vp"), q0, c2 / c1, ALU.is_gt, ALU.add)
    eq(ap("tt2"), ap("vb"), u112, c1)
    tt(ap("tt1"), ap("tt1"), ap("tt2"), ALU.mult)
    tt(ap("tri"), ap("tt1"), ap("idf"), ALU.add)
    ts(cols("v16", 0, nv), cols("v16", 0, nv), 127, None, ALU.bitwise_and)
    ts(cols("vg", 0, nv), cols("v16", 0, nv), 4, None, ALU.arith_shift_right)

    def blkw(buf, j):
        return cols(buf, 64 + 128 * j, 128 + 128 * j)

    def win(buf, j, h, p=ALL):
        a = 128 * j + 64 * (1 - h)
        return cols(buf, a, a + 128, p=p)

    for s_ in (0, 1):
        v = cols("v16", 64 * s_, 64 * s_ + 64)
        eq(blkw("wf", s_), v, q0, 1)
        eq(blkw("wb", s_), v, q0, R); eq(blkw("wb", 2 + s_), v, q0, -32 * R); eq(blkw("wb", 4 + s_), v, q0, 0.5)
        eq(cols("wf", 64 + 128 * (2 + s_), 128 + 128 * (2 + s_), p=p24), cols("vg", 64 * s_, 64 * s_ + 64, p=p24), ap("uf", p24, slice(1, 2)), 1)
        eq(blkw("wb", 6 + s_), cols("vp", 64 * s_, 64 * s_ + 64), q0, 0.5)
    eq(blkw("wf", 4), cols("vp", 0, 64), u63, 1)
    if rolled[0]:
        iota(cols("vj", 0, 64), [[-32, 2], [1, 32]], 32, 0)
        eq(blkw("wf", 5), cols("vj", 0, 64), u63, 1)
    for k in range(16):
        eq(cols("pen", 128 * k, 128 * k + 128), ap("vb"), cols("uq", k, k + 1), -4)
    sel(cols("rep", 0, 256), ap("one"), [[-64, 2], [0, 2], [-1, 64]], ALU.is_equal, 0.0, 0, 1)
    if any(rolled):
        sel(cols("rep", 256, 384), cols("one", 0, 128), [[-64, 2], [32, 2], [-1, 32]], ALU.is_equal, 0.0, -32, 1)
    for j in range(nv // 64):
        for h in (0, 1):
            ts(cols("v3", 128 * j + 64 * h, 128 * j + 64 * h + 64, p=p24), cols("vg", 64 * j, 64 * j + 64, p=p24), 3.0, None, ALU.mult)
        for l in range(3):
            eq(cols("dsel", 128 * (3 * j + l), 128 * (3 * j + l + 1), p=p24), cols("v3", 128 * j, 128 * j + 128, p=p24),
               ap("uq", p24, slice(l, l + 1)), 1)
    iota(ap("rst0"), [[0, HE], [256, NS]], 0, 0)["after"] = [i for i, o in enumerate(ops) if o["kind"] == "r"]
    act(ap("rst1"), ap("rst0"), AF.Copy)
    if CAP:
        for s_ in (0, 1):
            mset(slot("sl%d" % s_, NW + 1), 0.0)
    for h in (0, 1):
        iota(ap("ec", slice(64 * h, 64 * h + 64), ALL), [[1, HE]], V + 2 * E + HE * h, 0)
    cp(ap("dlb", p24, ALL), ap("dln", p24, ALL))
    cp(ap("nxf"), ap("nxn"))
    ts(ap("c3f", p24, ALL), ap("c3n", p24, ALL), ap("ab", p24, slice(0, 1)), ap("ab", p24, slice(4, 5)), ALU.mult, ALU.min)
    p1 = slice(0, 1)
    ones = cols("one", 0, HE, p=p1)
    cp(ap("ffn"), ap("fdn"))
    act(ap("ngn"), ap("ffn"), AF.Relu, scale=-1.0)
    p2 = slice(0, 2)
    mset(cols("cst", 256, 384, p=p2), R)
    sel(cols("cst", 256, 384, p=p2), cols("cst", 256, 384, p=p2), [[0, 128]], ALU.is_gt, -1.0, 1, -1)
    eq(ap("idk"), ap("vp"), q0, 1.0 / KF); eq(ap("prb"), ap("vp"), q0, R)

    def tmp(s_, j):
        return cols("ps%d" % (5 + s_), HE * j, HE * j + HE)

    def half(buf, l, h, base=0, p=ALL):
        a = base + E * l + HE * h
        return cols(buf, a, a + HE, p=p)

    def pack_rows(s_, l):
        q = cols("q%d" % s_, HE * l, HE * l + HE)
        if l == 0:
            t = tmp(s_, 1)
            mm([(t, win("wf", s_, h), half("ffn", l, h)) for h in (0, 1)] + [(t, win("wb", s_, h), half("pwn", l, h)) for h in (0, 1)]
               + [(t, win("wb", 2 + s_, h), half("ngn", l, h)) for h in (0, 1)] + [(t, cols("cst", 0, 128, p=p1), ones)])
            act(q, t, AF.Relu)
        else:
            t = cols("ps7", HE, E)
            a = HE * (2 * s_ + l - 1)
            kf = cols("kf", a, a + HE)
            ts(kf, cols("fds", a, a + HE), 1.0, KF, ALU.add, ALU.mult)
            mm([(t, ap("idk"), kf), (t, ap("prb"), cols("pws", a, a + HE)), (t, cols("cst", 256, 384, p=p2), cols("one", 0, HE, p=p2))])
            tt(q, kf, t, ALU.min)

    def base(rd, l, s_):
        if BP16:
            p96 = slice(0, 96)

            def piece(buf, h, j):
                a = E * l + HE * h + 96 * j
                return cols(buf, a, a + 96)

            terms = []
            for j in (0, 1):
                t = cols("ps7", 128 * j, 128 * j + 128, p=p96)
                terms += ([(t, piece("bsn", h, j), win("wb", 4 + s_, h)) for h in (0, 1)]
                          + [(t, piece("wa%d" % s_, h, j), win("wb", 6 + h, h)) for h in (0, 1)]
                          + [(t, cols("one", 0, 96, p=p1), cols("cst", 128, 256, p=p1))])
            mm(terms, each=5)
            bt = ap("bt", p96, ALL)
            ts(bt, cols("ps7", 0, 256, p=p96), MAGIC, MAGIC, ALU.add, ALU.subtract)
            outs = [cols("ps3", HE * s_ + 96 * j, HE * s_ + 96 * j + 96) for j in (0, 1)]
            add("P", [("transpose", (outs[j], cols("bt", 128 * j, 128 * j + 128, p=p96), cols("ib", 0, 96, p=p96)), {}) for j in (0, 1)],
                [bt, ap("ib")], outs, work(pi=2, pe=256))
            act(slot("sl%d" % s_, NW), cols("ps3", HE * s_, HE * s_ + HE), AF.Copy)
            return
        t = cols("ps7", 0, HE)
        mm([(t, win("wb", 4 + s_, h), half("bsn", l, h)) for h in (0, 1)]
           + [(t, win("wb", 6 + h, h), half("wa%d" % s_, l, h)) for h in (0, 1)] + [(t, cols("cst", 128, 256, p=p1), ones)])
        b = slot("sl%d" % s_, NW)
        if B_ACT:
            act(t, t, AF.Identity, bias=MAGIC)
            act(b, t, AF.Identity, bias=-MAGIC)
        else:
            ts(b, t, MAGIC, MAGIC, ALU.add, ALU.subtract)
        mm([(cols("ps3", HE * s_, HE * s_ + HE), ap("ib"), b)])
        if CAP:
            j = 3 * s_ + l
            mm([(cols("ps7", 0, E), cols("dsel", 128 * j, 128 * j + 128, p=p24), ap("dlb", p24, ALL))])
            for h in (0, 1):
                ph = slice(64 * h, 64 * h + 64)
                act(cols("rst%d" % s_, NW + 1, HE * NS, NS, p=ph), cols("ps7", HE * h, HE * h + HE, p=ph), AF.Identity, bias=255.0, scale=-1.0)

    def places(s_):
        for l in range(3):
            t = cols("ps7", 12 * l, 12 * l + 12)
            mm([(t, win("wf", s_, h), cols("nxf", 24 * l + 12 * h, 24 * l + 12 * h + 12)) for h in (0, 1)])
        cp(ap("nxo%d" % s_), cols("ps7", 0, 36))
        act(ap("sc%d" % s_), ap("bsn"), AF.Identity, scale=0.0)

    mb = [0]

    def stage(rd, l, s_):
        n = lambda x: ap("%s%d" % (x, s_))
        wname = ("wa%d" if rd == 0 else "wc%d") % s_
        q = cols("q%d" % s_, HE * l, HE * l + HE)
        final = rd == 1 and l == 2
        t0_, t1_ = tmp(s_, 0), tmp(s_, 1)
        arr = None
        qn = n("qn")
        if QDMA:
            qb = cols("qb%d" % s_, HE * l, HE * l + HE)
            q, qn = (q, qb) if rd == 0 else (qb, qn)
        act(n("en"), q, AF.Exp, bias=LNK, scale=-CL / R)
        if rd == 1 and l == 0:
            iq = n("iz"); arr = 2 + s_
            act(n("ei"), iq, AF.Exp, bias=LNK + math.log(ALPHA), scale=-CL / R, arr=arr)
        else:
            iq = n("iq")
            if l == 0:
                mm([(t0_, win("wf", 2 + s_, h, p=p24), half("c3f", 0, h, p=p24)) for h in (0, 1)] + [(t0_, cols("cst", 0, 128, p=p1), ones)])
                act(iq, t0_, AF.Relu)
                act(n("ei"), iq, AF.Exp, bias=LNK + math.log(ALPHA), scale=-CL / R)
            else:
                mm([(t0_, win("wf", 4, h), half("sc%d" % s_, l - 1, h)) for h in (0, 1)])
                act(n("ei"), t0_, AF.Exp, bias=LNK + math.log(ALPHA), scale=-CL / R)
                act(iq, t0_, AF.Copy)
        mm([(t1_, ap("tri"), n("en")), (t1_, ap("nib"), n("ei"))])
        tt(t1_, iq, t1_, ALU.min, arr=arr)
        tt(qn, q, t1_, ALU.max)
        if WN_V:
            ts(n("wn"), qn, 1.0 / R, 128.0, ALU.mult, ALU.add)
        else:
            act(n("wn"), qn, AF.Identity, bias=128.0, scale=1.0 / R)
        if ED_V and not final:
            act(n("ep"), n("wn"), AF.Exp, bias=-128 * CL + K2 - math.log(64.0), scale=CL)
        mm([(t0_, ap("idf"), qn), (t0_, ap("nrb"), n("wn"))])
        ts(n("of"), t0_, 128 * R, None, ALU.add)
        if not final:
            mm([(t1_, ap("blk"), q), (t1_, ap("nblk"), qn), (t1_, ap("idf"), iq)], arr=arr, after=[len(ops) - 1])
            act(n("hq"), t1_, AF.Copy)
            act(n("eh"), n("hq"), AF.Exp, bias=K2 + math.log(ALPHA), scale=CL / R)
        bp = cols("ps3", HE * s_, HE * s_ + HE)
        tag[0] = 6 * rd + 2 * l + s_
        w = HE // GCH
        for j in range(GCH):
            o = cols("ga%d" % s_, 16 * w * j, 16 * w * (j + 1))
            src = ind(ap(wname), cols("of%d" % s_, w * j, w * j + w))
            a_ = (s_ if rd == 0 else 2 + s_) if l == 0 else None
            if (6 * rd + 2 * l + s_, j) in VGATHER:
                cp(o, src, arr=a_)
            else:
                act(o, src, AF.Copy, arr=a_)
        if rd == 0 and l < 2:
            pack_rows(s_, l + 1)
        cn = cols("ps4", 0, HE)
        mm([(cn, ap("nib"), n("wn"))], last=False)
        edges = [0, CSPLIT, HE] if CSPLIT else [0, HE]
        for a, z in zip(edges, edges[1:]):
            for k in range(16 if z == HE else NSPLIT):
                a2 = a if k < NSPLIT else 0
                c = cols("cmp", HE * k + a2, HE * k + z)
                tt(c, cols("ga%d" % s_, 16 * a2 + k, 16 * z, 16), cols("ps3", HE * s_ + a2, HE * s_ + z), ALU.is_gt)
                if z == HE:
                    mm([(cn, cols("cwin", 15 - k, 143 - k), cols("cmp", HE * k, HE * k + HE))], first=False, last=(k == 15), acc=True)
        ts(n("dr"), cn, -128.5, 64.0, ALU.is_gt, ALU.mult)
        if not final:
            if ED_V:
                mm([(t0_, ap("ib"), n("ep"))])
                tt(n("ed"), n("dr"), t0_, ALU.mult)
            else:
                mm([(t0_, ap("ib"), n("wn")), (t0_, ap("ib"), n("dr"))])
                act(n("ed"), t0_, AF.Exp, bias=-192 * CL + K2, scale=CL)
            mm([(t1_, ap("tri"), n("ed")), (t1_, ap("nib"), n("eh"))])
            stay = rd == 0 and not QDMA
            gq_ = q if stay else n("gn")
            if NG_ACT:
                act(t1_, t1_, AF.Relu, scale=-1.0 if stay else 1.0)
                tt(gq_, qn, t1_, ALU.min)
            else:
                ts(t1_, t1_, 0.0, None, ALU.is_le if stay else ALU.is_gt)
                tt(gq_, qn, t1_, ALU.mult)
            mm([(t0_, ap("blk"), qn), (t0_, ap("nblk"), q)] if stay else [(t0_, ap("blk"), gq_)])
            if rd == 0 and QDMA:
                act(q, gq_, AF.Copy, scale=-1.0)
                dma("G", [(qn, q)], 100e3, accum=True)
            tt(n("ou"), n("hq"), t0_, ALU.max)
            tgt = ind(cols("sc%d" % s_, E * l, E * l + E), cols("nxo%d" % s_, 12 * l, 12 * l + 12))
            if l < 2:
                cp(tgt, n("ou"))
            else:
                act(n("wo"), n("ou"), AF.Identity, bias=128.0, scale=1.0 / R)
                act(n("rw"), n("wo"), AF.Identity, bias=-128 * R, scale=R)
                tt(tgt, n("rw"), ap("ec"), ALU.add)
                mm([(t1_, win("wf", 5 if rolled[0] else 4, h), half("sc%d" % s_, 2, h)) for h in (0, 1)])
                act(n("isd"), t1_, AF.Copy)
                remote([(0, n("isd"), n("iz"))], 2 + s_, 100e3)
        for j in ORDER:
            bank = "ps%d" % (mb[0] % 3); mb[0] += 1
            ks = (2 * j, 2 * j + 1)
            outs = [cols(bank, i, E, 2) if PAIR else cols(bank, HE * i, HE * i + HE) for i in (0, 1)]
            if 2 * j < NX:
                for i in (0, 1):
                    o = cols(bank, HE * i, HE * i + HE)
                    mm([(o, cols("pen", 128 * ks[i], 128 * ks[i] + 128), n("dr"))])
                for i in (0, 1):
                    tt(slot("sl%d" % s_, ks[i]), cols("ga%d" % s_, ks[i], 3072, 16), cols(bank, HE * i, HE * i + HE), ALU.add)
                continue
            mm([x for i in (0, 1) for x in ((outs[i], ap("ib"), cols("ga%d" % s_, ks[i], 3072, 16)),
                                            (outs[i], cols("pen", 128 * ks[i], 128 * ks[i] + 128), n("dr")))], each=2)
            for src, sj, m in ([(cols(bank, 0, E), 2 * j % NW, 2)] if PAIR else [(outs[i], ks[i] % NW, 1) for i in (0, 1)]):
                d = slot("sl%d" % s_, sj, m)
                if 2 * j < NW:
                    act(d, src, AF.Copy)
                else:
                    tt(d, d, src, ALU.max)
        add("V", [("tensor_tensor_scan", (n("so"), n("rst"), n("sl"), 0.0, ALU.min, ALU.max), {})], [n("rst"), n("sl")], [n("so")],
            work(vi=1, cyc=0.5 * HE * NS))
        m_ = slot("so%d" % s_, NS - 1)
        t = cols("ps7", 0, E)
        j = 3 * s_ + l
        mm([(t, cols("dsel", 128 * j, 128 * j + 128, p=p24), ap("dlb", p24, ALL))]
           + [(cols("ps7", HE * h, HE * h + HE), cols("rep", 128 * h, 128 * h + 128), m_) for h in (0, 1)])
        if CAP:
            act(cols(wname, E * l, E * l + E), t, AF.Copy)
        else:
            ts(cols(wname, E * l, E * l + E), t, 255.0, None, ALU.min)
        if rd == 0 and any(rolled):
            mm([(t, cols("rep", 256, 384), cols(wname, E * l, E * l + E))])
            act(cols("rb%d" % s_, E * l, E * l + E), t, AF.Copy)
        if not final:
            base(rd + (l == 2), (l + 1) % 3, s_)
        if rd == 0:
            remote([(w_, cols(("rb%d" if rolled[w_] else "wa%d") % s_, E * l, E * l + E),
                     cols("wc%d" % s_, V * (w_ + 1) + E * l, V * (w_ + 1) + E * l + E)) for w_ in (0, 1)], 2 + s_, 200e3)
        else:
            dma("S", [(ap("yt", slice(16 * gq, 16 * (gq + c), None), slice(E * l, E * l + E)),
                       ap(wname, slice(16 * s, 16 * (s + c)), slice(E * l, E * l + E))) for s, gq, c in runs(s_, 0)], 50e3)

    for s_ in (0, 1):
        pack_rows(s_, 0)
        base(0, 0, s_)
    for s_ in (0, 1):
        places(s_)
    for rd in (0, 1):
        for l in range(3):
            for s_ in (0, 1):
                tag[0] = max(0, 6 * rd + 2 * l + s_ - 2)
                stage(rd, l, s_)
    return ops, arr_total


START = [{}, 0.08, 0.06, 10.0]


def schedule(ops):
    n = len(ops)
    hist = {}
    sends = {}
    for i, o in enumerate(ops):
        deps = set()
        for regs, is_w in ((o["rd"], False), (o["wr"], True)):
            for r in regs:
                for j, w, r2 in hist.get(r[0], ()):
                    if (w or is_w) and r[1] < r2[2] and r2[1] < r[2] and r[3] & r2[3]:
                        deps.add(j)
        for r in o["wr"]:
            hist[r[0]] = [x for x in hist.get(r[0], []) if not (r[1] <= x[2][1] and x[2][2] <= r[2] and (x[2][3] & ~r[3]) == 0)]
        for r in o["wr"]:
            hist[r[0]].append((i, True, r))
        for r in o["rd"]:
            hist.setdefault(r[0], []).append((i, False, r))
        deps.discard(i)
        o["deps"] = deps
        o["soft"] = set(sends.get(o["arr"], ())) if o["arr"] is not None else set()
        o["soft"] |= set(o.get("after", ()))
        if o["kind"] == "r":
            sends.setdefault(o["sends"], []).append(i)
    succ = [[] for _ in ops]
    left = [0] * n
    for i, o in enumerate(ops):
        for j in o["deps"] | o["soft"]:
            succ[j].append(i); left[i] += 1
    eng = [o["eng"] for o in ops]
    banks = [sorted(o["banks"]) for o in ops]
    pred = [[(k, not (o["acc"] and eng[k] == "P")) for k in sorted(o["deps"] | o["soft"])] for o in ops]
    costs = [([float(o["cost"] @ w) for o in ops], [float(o["hold"] @ w) for o in ops], lat) for w, lat in RATES]

    def place(boost, thr, frac, lead):
        cost, hold, lat = costs[0]
        prio = [0.0] * n
        for i in range(n - 1, -1, -1):
            prio[i] = cost[i] + lat + max([prio[j] for j in succ[i]], default=0.0)
        prio = [p + boost[i] - lead * ops[i]["tag"] for i, p in enumerate(prio)]
        free = dict.fromkeys("VAPGS", 0.0)
        bank = {}
        lf = list(left)
        dep_t = [0.0] * n
        end = [0.0] * n
        extra = [()] * n
        ready = [i for i in range(n) if lf[i] == 0]
        order = []
        while ready:
            st = []
            for i in ready:
                t = max(free[eng[i]], dep_t[i])
                for b in banks[i]:
                    for e, j in bank.get(b, {}).items():
                        if e != eng[i] and end[j] + lat > t:
                            t = end[j] + lat
                st.append((t, i))
            t, i0 = min(st)
            lim = t + thr + frac * hold[i0]
            p, i, t = max((prio[i], -i, s) for s, i in st if eng[i] == eng[i0] and s <= lim)
            i = -i
            end[i] = t + cost[i]
            free[eng[i]] = t + hold[i]
            ex = []
            for b in banks[i]:
                ex += [j for e, j in bank.get(b, {}).items() if e != eng[i]]
                bank.setdefault(b, {})[eng[i]] = i
            extra[i] = ex
            order.append(i); ready.remove(i)
            for j in succ[i]:
                lf[j] -= 1
                if lf[j] == 0:
                    dep_t[j] = max(end[k] + (lat if w else 0.0) for k, w in pred[j])
                    ready.append(j)
        return order, extra

    def span(order, extra, m):
        cost, hold, lat = costs[m]
        free = dict.fromkeys("VAPGS", 0.0)
        end = [0.0] * n
        beg = [0.0] * n
        for i in order:
            t = free[eng[i]]
            for k, w in pred[i]:
                t = max(t, end[k] + (lat if w else 0.0))
            for k in extra[i]:
                t = max(t, end[k] + lat)
            beg[i] = t
            end[i] = t + cost[i]
            free[eng[i]] = t + hold[i]
        return max(end), beg

    state = [12345]

    def rnd():
        state[0] = (state[0] * 1103515245 + 12345) % 2147483648
        return state[0] / 2147483648.0

    by = {}
    for i, o in enumerate(ops):
        name = o["wr"][0][0].rstrip("01") if o["wr"] else ""
        by.setdefault((eng[i], name, -1), []).append(i)
        by.setdefault((eng[i], name, o["tag"]), []).append(i)
    kinds = sorted(by)
    wide = [k for k in kinds if k[2] == -1]
    best = None
    for k in range(TRIES if START[0] else int(2.5 * TRIES)):
        if k == 0:
            trial = (dict(START[0]),) + tuple(START[1:])
        else:
            b0, thr, frac, lead = best[3]
            b1 = dict(b0)
            for _ in range(1 + int(2 * rnd())):
                pool = wide if rnd() < 0.3 else kinds
                pick = pool[int(rnd() * len(pool))]
                b1[pick] = round(b1.get(pick, 0.0) + 16 * rnd() * (rnd() - 0.5), 1)
            if rnd() < 0.1:
                thr, frac = max(0.0, round(thr + 0.1 * (rnd() - 0.5), 2)), min(1.0, max(0.0, round(frac + 0.3 * (rnd() - 0.5), 2)))
            trial = (b1, thr, frac, round(lead + (4 * rnd() - 2 if rnd() < 0.1 else 0.0), 1))
        boost = [0.0] * n
        for key, x in trial[0].items():
            for i in by.get(key, ()):
                boost[i] += x
        order, extra = place(boost, *trial[1:])
        sp = [span(order, extra, m)[0] for m in range(len(RATES))]
        score = sp[0] + 0.6 * sp[1] + 0.4 * sp[2]
        if best is None or score <= best[0]:
            best = (score, order, extra, trial, sp)
    START[:] = best[3]
    beg = span(best[1], best[2], 0)[1]
    for i, o in enumerate(ops):
        o["deps"] |= set(best[2][i])
        o["start"] = beg[i]; o["end"] = beg[i] + costs[0][0][i]; o["held"] = costs[0][1][i]
    ops[0]["spans"] = best[4]
    return best[1]


def rank_program(g, core, T, topo):
    rank = T.rank_of(core)
    if rank is None:
        return
    ops, arr_total = build(rank, core, list(T.cores), topo)
    order = schedule(ops)
    queue = {"V": g.vector, "A": g.scalar, "P": g.tensor, "G": g, "S": g.sync}
    method = {
        "tensor_scalar": g.vector.tensor_scalar, "tensor_tensor": g.vector.tensor_tensor, "tensor_copy": g.vector.tensor_copy,
        "memset": g.vector.memset, "tensor_tensor_scan": g.vector.tensor_tensor_scan, "activation": g.scalar.activation,
        "matmul": g.tensor.matmul, "transpose": g.tensor.transpose, "iota": g.iota, "affine_select": g.affine_select}

    def real(a):
        if isinstance(a, tuple) and a[0] == "ap":
            return T[a[1]][a[2]]
        if isinstance(a, tuple) and a[0] == "ind":
            return real(a[1]).indirect(real(a[2]))
        return a

    needed = set()
    for o in ops:
        needed |= set(j for j in o["deps"] if not (o["acc"] and ops[j]["eng"] == "P"))
    count = dict.fromkeys("VAPG", 0)
    known = {e: {} for e in "VAPGS"}
    totals = {}

    def wait(e, sem, val):
        if known[e].get(sem, 0) < val:
            queue[e].wait_ge(T.sem[sem], val)
            known[e][sem] = val

    for i in order:
        o = ops[i]; e = o["eng"]
        need = {}
        for j in o["deps"]:
            if o["acc"] and ops[j]["eng"] == "P":
                continue
            sem, val = ops[j]["sig"]
            need[sem] = max(need.get(sem, 0), val)
        if e == "G" and o["kind"] == "c":
            needed.add(i)
            need["eG"] = count["G"]
        if o["arr"] is not None:
            need["arr%d" % o["arr"]] = arr_total[o["arr"]]
        for sem in sorted(need):
            wait(e, sem, need[sem])
        if o["kind"] == "r":
            tr = [RemoteDMATransfer(dst_ids=[DstId(rid=a[0], pnc=a[1])], dma_engine_mask=m, remote_sem=T.sem[o["rsem"]],
                                    src=real(s), dst=real(d)) for a, m, s, d in o["calls"][0][1]]
            g.remote_dma_fused(tr, local_sem=T.sem[o["sem"]])
            o["sig"] = (o["sem"], o["total"])
        elif o["kind"] == "d":
            for _, args, _k in o["calls"]:
                queue[e].dma_start(real(args[0]), real(args[1]), **_k).then_inc(T.sem[o["sem"]], 16)
            o["sig"] = (o["sem"], o["total"])
        else:
            ins = None
            for name, args, kw in o["calls"]:
                ins = method[name](*[real(a) for a in args], **kw)
            if i in needed:
                count[e] += 1
                ins.then_inc(T.sem["e" + e], 1)
            o["sig"] = ("e" + e, count[e])
        totals[o["sig"][0]] = max(totals.get(o["sig"][0], 0), o["sig"][1])
    for k in range(4):
        totals["arr%d" % k] = arr_total[k]
    for sem in sorted(totals):
        if totals[sem] > 0 and max(known[e].get(sem, 0) for e in known) < totals[sem]:
            wait("S", sem, totals[sem])
